import numpy as np
import ml_dtypes


def mxq(x, axis, fmt="e4m3"):
    dtype, down = {"e4m3": (ml_dtypes.float8_e4m3fn, 7), "e5m2": (ml_dtypes.float8_e5m2, 14)}[fmt]
    v = np.moveaxis(np.asarray(x, np.float32).astype(ml_dtypes.bfloat16).astype(np.float64), axis, -1)
    blocks = v.reshape(v.shape[:-1] + (-1, 32))
    amax = np.abs(blocks).max(-1, keepdims=True)
    byte = np.maximum(np.where(amax > 0, np.frexp(amax)[1] - 1 + 127, 0) - down, 1)
    scale = np.exp2(byte - 127.0)
    codes = (blocks / scale).astype(np.float32).astype(dtype).astype(np.float64)
    return np.moveaxis((codes * scale).reshape(v.shape), -1, axis)


WIDE = False


def mx_kscale(k):
    if not WIDE:
        return np.ones(k)
    levels = np.array([18, -18])
    if k % 512:
        return np.exp2(np.random.permutation(np.resize(levels, k // 32))).repeat(32)
    a = np.empty((k // 512, 16))
    for p in range(k // 512):
        a[p, :8] = np.random.permutation(np.resize(levels, 8))
        for g in range(8):
            far = levels[np.abs(levels - a[p, g]) >= 10]
            a[p, g + 8] = far[np.random.randint(len(far))]
    return np.exp2(a.ravel()).repeat(32)


def f64(x):
    return np.asarray(x).astype(np.float64)


def striped(idx):
    return np.tile(np.asarray(idx).reshape(-1, 16).T, (8, 1)).astype(np.uint16)


def unstriped(offs):
    return offs[:16].T.reshape(-1).astype(np.int64)


V, E, D, DV = 512, 2048, 512, 1024


def setup_inputs():
    n = np.random.standard_normal
    u = mx_kscale(E)
    coarse = lambda x: x.astype(np.float32).astype(ml_dtypes.bfloat16).astype(np.float64)
    return {
        "xT": (coarse(n((D, V)))).astype(np.float32),
        "dyT": (coarse(n((DV, V)))).astype(np.float32),
        "sw": np.tile(np.random.randint(8, 33, E) / 512.0 / u, (128, 1)).astype(np.float32),
        "tw": np.tile(np.random.randint(8, 33, E) / 16.0 * u, (128, 1)).astype(np.float32),
        "offs": striped(np.random.randint(0, V, E)),
        "offs2": striped(np.random.randint(0, V, E)),
    }


def reference(xT, dyT, sw, tw, offs, offs2):
    xe = f64(sw)[:1] * f64(xT)[:, unstriped(offs)]
    dz = f64(tw)[:1] * f64(dyT)[:, unstriped(offs2)]
    return mxq(xe, 1, "e4m3") @ mxq(dz, 1, "e5m2").T

@@ -1,0 +1,173 @@
+from contextlib import ExitStack
+
+import concourse.mybir as mybir
+from concourse.masks import make_identity
+
+V, E, D, DV = 512, 2048, 512, 1024
+FLOPS = 2 * E * D * DV
+
+F32 = mybir.dt.float32
+BF16 = mybir.dt.bfloat16
+U32 = mybir.dt.uint32
+U16 = mybir.dt.uint16
+U8 = mybir.dt.uint8
+E4M3 = mybir.dt.float8_e4m3fn_x4
+E5M2 = mybir.dt.float8_e5m2_x4
+MULT = mybir.AluOpType.mult
+
+P = 128
+PASS = 512
+PASSES = E // PASS
+N_TILE = 512
+SPARE = 16
+LIST_COLS = PASS // 16
+
+
+def tile_attend_gmw_kernel(tc, xT, dyT, sw, tw, offs, offs2, out):
+    nc = tc.nc
+    x_blocks = D // P
+    dy_blocks = DV // P
+    halves = DV // N_TILE
+    per_half = N_TILE // P
+
+    with ExitStack() as ctx:
+        keep = ctx.enter_context(tc.tile_pool(name="keep", bufs=1))
+        ring = ctx.enter_context(tc.tile_pool(name="ring", bufs=4))
+        turn = ctx.enter_context(tc.psum_pool(name="turn", bufs=4))
+        sums = ctx.enter_context(tc.psum_pool(name="sums", bufs=2))
+
+        src = keep.tile([P, E // 16], U16, name="src")
+        dst = keep.tile([P, E // 16], U16, name="dst")
+        x_win = [keep.tile([P, V + SPARE], F32, name="x_win%d" % j) for j in range(x_blocks)]
+        dy_win = [keep.tile([P, V + SPARE], F32, name="dy_win%d" % j) for j in range(dy_blocks)]
+        tw_first = keep.tile([P, PASS], F32, name="tw_first")
+        tw_rest = keep.tile([P, E - PASS], F32, name="tw_rest")
+        sw_all = keep.tile([P, E], F32, name="sw_all")
+        ident = keep.tile([P, P], F32, name="ident")
+
+        nc.sync.dma_start(dst[:], offs2)
+        nc.sync.dma_start(dy_win[0][:, :V], dyT[0:P, :])
+        nc.sync.dma_start(tw_first[:], tw[:, :PASS])
+        for j in range(1, per_half):
+            nc.sync.dma_start(dy_win[j][:, :V], dyT[j * P : (j + 1) * P, :])
+        nc.sync.dma_start(tw_rest[:], tw[:, PASS:])
+        for j in range(per_half, dy_blocks):
+            nc.sync.dma_start(dy_win[j][:, :V], dyT[j * P : (j + 1) * P, :])
+        nc.sync.dma_start(src[:], offs)
+        for j in range(x_blocks):
+            nc.sync.dma_start(x_win[j][:, :V], xT[j * P : (j + 1) * P, :])
+        nc.sync.dma_start(sw_all[:], sw)
+        for window in dy_win + x_win:
+            nc.gpsimd.memset(window[:, V:], 0.0)
+        make_identity(nc, ident[:])
+
+        def weights(g, on_dy):
+            if not on_dy:
+                return sw_all[:, g * PASS : (g + 1) * PASS]
+            if g == 0:
+                return tw_first[:]
+            return tw_rest[:, (g - 1) * PASS : g * PASS]
+
+        def gather(window, offsets, g, on_dy):
+            picked = ring.tile([P, PASS], F32, name="picked")
+            nc.vector.tensor_tensor(
+                picked[:],
+                window[:].indirect(offsets[:, g * LIST_COLS : (g + 1) * LIST_COLS]),
+                weights(g, on_dy),
+                MULT,
+            )
+            return picked
+
+        def round_pairs(picked):
+            rounded = ring.tile([P, PASS], BF16, name="rounded")
+            nc.scalar.copy(
+                rounded[:].rearrange("f (u q r) -> f u q r", u=2, r=16),
+                picked[:].rearrange("f (q u r) -> f u q r", u=2, r=16),
+            )
+            return rounded
+
+        def turn_pairs(rounded_list):
+            bank = turn.tile([P, 4, P], F32, name="bank")
+            for s, rounded in enumerate(rounded_list):
+                words = rounded[:].bitcast(F32)
+                for u in range(2):
+                    nc.tensor.transpose(bank[:, 2 * s + u, :], words[:, u * P : (u + 1) * P], ident[:])
+            return bank
+
+        def weave(bank, count, grouped, first):
+            words = grouped[:, first * PASS : (first + count) * PASS].bitcast(F32)
+            nc.scalar.copy(
+                words.rearrange("p (s c u) -> p s c u", s=count, u=2),
+                bank[:, : 2 * count, :].rearrange("p (s u) c -> p s c u", u=2),
+            )
+
+        dy_codes = {}
+        dy_scales = {}
+        x_codes = {}
+        x_scales = {}
+        steps = []
+        for h in range(halves):
+            for g in range(PASSES):
+                dy_codes[h, g] = keep.tile([P, N_TILE], U32, name="dy_codes%d_%d" % (h, g), align_bytes=64)
+                dy_scales[h, g] = keep.tile([P, N_TILE], U8, name="dy_scales%d_%d" % (h, g), align_bytes=64)
+                steps.append(
+                    ([(dy_win[h * per_half + j], dst, g, True) for j in range(per_half)], dy_codes[h, g], dy_scales[h, g], E5M2, None)
+                )
+        for j in range(x_blocks):
+            groups = [list(range(PASSES))] if j < x_blocks - 1 else [[0, 1], [2], [3]]
+            for group in groups:
+                codes = keep.tile([P, len(group) * P], U32, name="x_codes%d_%d" % (j, group[0]), align_bytes=64)
+                scales = keep.tile([P, len(group) * P], U8, name="x_scales%d_%d" % (j, group[0]), align_bytes=64)
+                for i, g in enumerate(group):
+                    x_codes[j, g] = codes[:, i * P : (i + 1) * P]
+                    x_scales[j, g] = scales[:, i * P : (i + 1) * P]
+                steps.append(([(x_win[j], src, g, False) for g in group], codes, scales, E4M3, (j, group)))
+
+        acc = {}
+
+        def prepare(step):
+            units = step[0]
+            grouped = ring.tile([P, 4 * PASS], BF16, name="grouped", align_bytes=64, bufs=3)
+            for first in range(0, len(units), 2):
+                pair = units[first : first + 2]
+                rounded_list = [round_pairs(gather(*unit)) for unit in pair]
+                weave(turn_pairs(rounded_list), len(pair), grouped, first)
+            return grouped
+
+        def finish(step, grouped):
+            units, codes, scales, fmt, product = step
+            nc.vector.quantize_mx(out=codes[:].bitcast(fmt), scales=scales[:], in_=grouped[:, : len(units) * PASS])
+            if product is None:
+                return
+            j, group = product
+            for h in range(halves):
+                if group[0] == 0:
+                    acc[h] = sums.tile([P, N_TILE], F32, name="acc%d" % h)
+            for g in group:
+                for h in range(halves):
+                    nc.tensor.matmul_mx(
+                        out=acc[h][:],
+                        lhsT=x_codes[j, g].bitcast(E4M3),
+                        lhsT_scale=x_scales[j, g],
+                        rhs=dy_codes[h, g][:].bitcast(E5M2),
+                        rhs_scale=dy_scales[h, g][:],
+                        start=(g == 0),
+                        stop=(g == PASSES - 1),
+                    )
+            if group[-1] != PASSES - 1:
+                return
+            for h in range(halves):
+                result = ring.tile([P, N_TILE], F32, name="result")
+                if j == x_blocks - 1 and h == 0:
+                    nc.vector.tensor_copy(result[:], acc[h][:])
+                else:
+                    nc.scalar.copy(result[:], acc[h][:])
+                nc.sync.dma_start(out[j * P : (j + 1) * P, h * N_TILE : (h + 1) * N_TILE], result[:])
+
+        waiting = None
+        for step in steps:
+            grouped = prepare(step)
+            if waiting is not None:
+                finish(*waiting)
+            waiting = (step, grouped)
+        finish(*waiting)

@@ -20,7 +20,8 @@ PASS = 512
 PASSES = E // PASS
 N_TILE = 512
 SPARE = 16
-LIST_COLS = PASS // 16
+FIRST_CUTS = (0, 512, 1024, 2048)
+LAG = 3
 
 
 def tile_attend_gmw_kernel(tc, xT, dyT, sw, tw, offs, offs2, out):
@@ -32,142 +33,147 @@ def tile_attend_gmw_kernel(tc, xT, dyT, sw, tw, offs, offs2, out):
 
     with ExitStack() as ctx:
         keep = ctx.enter_context(tc.tile_pool(name="keep", bufs=1))
-        ring = ctx.enter_context(tc.tile_pool(name="ring", bufs=4))
-        turn = ctx.enter_context(tc.psum_pool(name="turn", bufs=4))
-        sums = ctx.enter_context(tc.psum_pool(name="sums", bufs=2))
+        ring = ctx.enter_context(tc.tile_pool(name="ring", bufs=3))
+        turn = ctx.enter_context(tc.psum_pool(name="turn", bufs=2))
+        sums = ctx.enter_context(tc.psum_pool(name="sums", bufs=3))
+
+        dy_cuts = [FIRST_CUTS] + [(0, 2048)] * (dy_blocks - 1)
+
+        def window_tile(longest, name):
+            return keep.tile([P, max(V, longest) + SPARE], F32, name=name)
 
         src = keep.tile([P, E // 16], U16, name="src")
         dst = keep.tile([P, E // 16], U16, name="dst")
-        x_win = [keep.tile([P, V + SPARE], F32, name="x_win%d" % j) for j in range(x_blocks)]
-        dy_win = [keep.tile([P, V + SPARE], F32, name="dy_win%d" % j) for j in range(dy_blocks)]
-        tw_first = keep.tile([P, PASS], F32, name="tw_first")
-        tw_rest = keep.tile([P, E - PASS], F32, name="tw_rest")
+        x_win = [window_tile(2 * PASS, "x_win%d" % j) for j in range(x_blocks)]
+        dy_win = [
+            window_tile(max(b - a for a, b in zip(cuts, cuts[1:])), "dy_win%d" % j) for j, cuts in enumerate(dy_cuts)
+        ]
+        tw_all = keep.tile([P, E], F32, name="tw_all")
         sw_all = keep.tile([P, E], F32, name="sw_all")
         ident = keep.tile([P, P], F32, name="ident")
 
         nc.sync.dma_start(dst[:], offs2)
         nc.sync.dma_start(dy_win[0][:, :V], dyT[0:P, :])
-        nc.sync.dma_start(tw_first[:], tw[:, :PASS])
-        for j in range(1, per_half):
-            nc.sync.dma_start(dy_win[j][:, :V], dyT[j * P : (j + 1) * P, :])
-        nc.sync.dma_start(tw_rest[:], tw[:, PASS:])
-        for j in range(per_half, dy_blocks):
+        for a, b in zip(FIRST_CUTS, FIRST_CUTS[1:]):
+            nc.sync.dma_start(tw_all[:, a:b], tw[:, a:b])
+        for j in range(1, dy_blocks):
             nc.sync.dma_start(dy_win[j][:, :V], dyT[j * P : (j + 1) * P, :])
         nc.sync.dma_start(src[:], offs)
+        nc.sync.dma_start(sw_all[:], sw)
         for j in range(x_blocks):
             nc.sync.dma_start(x_win[j][:, :V], xT[j * P : (j + 1) * P, :])
-        nc.sync.dma_start(sw_all[:], sw)
-        for window in dy_win + x_win:
+        for n, window in enumerate(dy_win + x_win):
             nc.gpsimd.memset(window[:, V:], 0.0)
-        make_identity(nc, ident[:])
+            if n == 1:
+                make_identity(nc, ident[:])
 
-        def weights(g, on_dy):
-            if not on_dy:
-                return sw_all[:, g * PASS : (g + 1) * PASS]
-            if g == 0:
-                return tw_first[:]
-            return tw_rest[:, (g - 1) * PASS : g * PASS]
+        def gather(picked, window, offsets, weights, a, b):
+            nc.vector.tensor_tensor(picked, window[:].indirect(offsets[:, a // 16 : b // 16]), weights[:, a:b], MULT)
 
-        def gather(window, offsets, g, on_dy):
-            picked = ring.tile([P, PASS], F32, name="picked")
-            nc.vector.tensor_tensor(
-                picked[:],
-                window[:].indirect(offsets[:, g * LIST_COLS : (g + 1) * LIST_COLS]),
-                weights(g, on_dy),
-                MULT,
-            )
-            return picked
-
-        def round_pairs(picked):
-            rounded = ring.tile([P, PASS], BF16, name="rounded")
-            nc.scalar.copy(
-                rounded[:].rearrange("f (u q r) -> f u q r", u=2, r=16),
-                picked[:].rearrange("f (q u r) -> f u q r", u=2, r=16),
+        def round_once(picked, round_copy):
+            count = picked.shape[1] // PASS
+            rounded = ring.tile([P, 2 * PASS], BF16, name="rounded")
+            round_copy(
+                rounded[:, : count * PASS].rearrange("f (g u q r) -> f g u q r", g=count, u=2, r=16),
+                picked.rearrange("f (g q u r) -> f g u q r", g=count, u=2, r=16),
             )
             return rounded
 
-        def turn_pairs(rounded_list):
+        def turn_and_weave(rounded, count, target, weave_copy):
             bank = turn.tile([P, 4, P], F32, name="bank")
-            for s, rounded in enumerate(rounded_list):
-                words = rounded[:].bitcast(F32)
-                for u in range(2):
-                    nc.tensor.transpose(bank[:, 2 * s + u, :], words[:, u * P : (u + 1) * P], ident[:])
-            return bank
+            words = rounded[:].bitcast(F32)
+            for n in range(2 * count):
+                nc.tensor.transpose(bank[:, n, :], words[:, n * P : (n + 1) * P], ident[:])
+            weave_copy(target, bank[:, : 2 * count, :].rearrange("p (s u) c -> p s c u", u=2))
 
-        def weave(bank, count, grouped, first):
-            words = grouped[:, first * PASS : (first + count) * PASS].bitcast(F32)
-            nc.scalar.copy(
-                words.rearrange("p (s c u) -> p s c u", s=count, u=2),
-                bank[:, : 2 * count, :].rearrange("p (s u) c -> p s c u", u=2),
-            )
+        dy_codes = [keep.tile([P, PASSES * N_TILE], U32, name="dy_codes%d" % h, align_bytes=64) for h in range(halves)]
+        dy_scales = [keep.tile([P, PASSES * N_TILE], U8, name="dy_scales%d" % h, align_bytes=64) for h in range(halves)]
 
-        dy_codes = {}
-        dy_scales = {}
-        x_codes = {}
-        x_scales = {}
-        steps = []
-        for h in range(halves):
-            for g in range(PASSES):
-                dy_codes[h, g] = keep.tile([P, N_TILE], U32, name="dy_codes%d_%d" % (h, g), align_bytes=64)
-                dy_scales[h, g] = keep.tile([P, N_TILE], U8, name="dy_scales%d_%d" % (h, g), align_bytes=64)
-                steps.append(
-                    ([(dy_win[h * per_half + j], dst, g, True) for j in range(per_half)], dy_codes[h, g], dy_scales[h, g], E5M2, None)
+        def quantise_half(h, grouped):
+            width = 1024
+            for a in range(0, PASSES * N_TILE, width):
+                nc.vector.quantize_mx(
+                    out=dy_codes[h][:, a : a + width].bitcast(E5M2),
+                    scales=dy_scales[h][:, a : a + width],
+                    in_=grouped[:, 4 * a : 4 * (a + width)],
                 )
-        for j in range(x_blocks):
-            groups = [list(range(PASSES))] if j < x_blocks - 1 else [[0, 1], [2], [3]]
-            for group in groups:
-                codes = keep.tile([P, len(group) * P], U32, name="x_codes%d_%d" % (j, group[0]), align_bytes=64)
-                scales = keep.tile([P, len(group) * P], U8, name="x_scales%d_%d" % (j, group[0]), align_bytes=64)
-                for i, g in enumerate(group):
-                    x_codes[j, g] = codes[:, i * P : (i + 1) * P]
-                    x_scales[j, g] = scales[:, i * P : (i + 1) * P]
-                steps.append(([(x_win[j], src, g, False) for g in group], codes, scales, E4M3, (j, group)))
+
+        dy_grouped = []
+        for block in range(dy_blocks):
+            h, j = divmod(block, per_half)
+            if block == per_half + 2:
+                quantise_half(0, dy_grouped[0])
+            picked = ring.tile([P, E], F32, name="picked", bufs=2)
+            if j == 0:
+                dy_grouped.append(
+                    keep.tile([P, PASSES * 4 * N_TILE], BF16, name="dy_grouped%d" % h, tag="half%d" % h, align_bytes=64)
+                )
+            words = dy_grouped[h][:].bitcast(F32).rearrange("p (g j c u) -> p j g c u", g=PASSES, j=per_half, u=2)
+            cuts = dy_cuts[block]
+            for a, b in zip(cuts, cuts[1:]):
+                gather(picked[:, a:b], dy_win[block], dst, tw_all, a, b)
+            for g in (0, 2):
+                rounded = round_once(picked[:, g * PASS : (g + 2) * PASS], nc.scalar.copy)
+                turn_and_weave(rounded, 2, words[:, j, g : g + 2], nc.scalar.copy)
 
         acc = {}
 
-        def prepare(step):
-            units = step[0]
-            grouped = ring.tile([P, 4 * PASS], BF16, name="grouped", align_bytes=64, bufs=3)
-            for first in range(0, len(units), 2):
-                pair = units[first : first + 2]
-                rounded_list = [round_pairs(gather(*unit)) for unit in pair]
-                weave(turn_pairs(rounded_list), len(pair), grouped, first)
-            return grouped
-
-        def finish(step, grouped):
-            units, codes, scales, fmt, product = step
-            nc.vector.quantize_mx(out=codes[:].bitcast(fmt), scales=scales[:], in_=grouped[:, : len(units) * PASS])
-            if product is None:
-                return
-            j, group = product
-            for h in range(halves):
-                if group[0] == 0:
-                    acc[h] = sums.tile([P, N_TILE], F32, name="acc%d" % h)
-            for g in group:
+        def multiply(j, group, grouped):
+            width = len(group) * P
+            codes = ring.tile([P, 2 * P], U32, name="x_codes", align_bytes=64)
+            scales = ring.tile([P, 2 * P], U8, name="x_scales", align_bytes=64)
+            nc.vector.quantize_mx(out=codes[:, :width].bitcast(E4M3), scales=scales[:, :width], in_=grouped[:, : 4 * width])
+            if group[0] == 0:
+                acc[j] = [sums.tile([P, N_TILE], F32, name="acc%d" % h) for h in range(halves)]
+            for i, g in enumerate(group):
                 for h in range(halves):
                     nc.tensor.matmul_mx(
-                        out=acc[h][:],
-                        lhsT=x_codes[j, g].bitcast(E4M3),
-                        lhsT_scale=x_scales[j, g],
-                        rhs=dy_codes[h, g][:].bitcast(E5M2),
-                        rhs_scale=dy_scales[h, g][:],
+                        out=acc[j][h][:],
+                        lhsT=codes[:, i * P : (i + 1) * P].bitcast(E4M3),
+                        lhsT_scale=scales[:, i * P : (i + 1) * P],
+                        rhs=dy_codes[h][:, g * N_TILE : (g + 1) * N_TILE].bitcast(E5M2),
+                        rhs_scale=dy_scales[h][:, g * N_TILE : (g + 1) * N_TILE],
                         start=(g == 0),
                         stop=(g == PASSES - 1),
                     )
-            if group[-1] != PASSES - 1:
-                return
-            for h in range(halves):
-                result = ring.tile([P, N_TILE], F32, name="result")
-                if j == x_blocks - 1 and h == 0:
-                    nc.vector.tensor_copy(result[:], acc[h][:])
-                else:
-                    nc.scalar.copy(result[:], acc[h][:])
-                nc.sync.dma_start(out[j * P : (j + 1) * P, h * N_TILE : (h + 1) * N_TILE], result[:])
 
-        waiting = None
-        for step in steps:
-            grouped = prepare(step)
-            if waiting is not None:
-                finish(*waiting)
-            waiting = (step, grouped)
-        finish(*waiting)
+        def store(j):
+            for h in range(halves):
+                result = ring.tile([P, N_TILE], F32, name="result", bufs=4)
+                rows = out[j * P : (j + 1) * P, h * N_TILE : (h + 1) * N_TILE]
+                if j == x_blocks - 1:
+                    if h == 0:
+                        nc.vector.tensor_copy(result[:], acc[j][h][:])
+                    else:
+                        nc.scalar.copy(result[:], acc[j][h][:])
+                    nc.sync.dma_start(rows, result[:])
+                else:
+                    nc.scalar.copy(result[:], acc[j][h][:])
+                    nc.sync.dma_start(rows, result[:])
+
+        pieces = [(j, group) for j in range(x_blocks - 1) for group in ((0, 1), (2, 3))]
+        pieces = pieces + [(x_blocks - 1, group) for group in ((0,), (1,), (2,), (3,))]
+        waiting = []
+        for k, (j, group) in enumerate(pieces):
+            slot = "piece%d" % k
+            if k == 3:
+                quantise_half(1, dy_grouped[1])
+            if k > LAG:
+                multiply(*waiting[k - LAG - 1])
+            count = len(group)
+            if k in ():
+                picked = keep.tile([P, 2 * PASS], F32, name="x_picked%d" % k, tag="piece%d" % (k - LAG - 1), align_bytes=64)
+            else:
+                picked = ring.tile([P, E], F32, name="picked", bufs=2)
+            gather(picked[:, : count * PASS], x_win[j], src, sw_all, group[0] * PASS, (group[-1] + 1) * PASS)
+            last = k == len(pieces) - 1
+            rounded = round_once(picked[:, : count * PASS], nc.vector.tensor_copy if last else nc.scalar.copy)
+            grouped = keep.tile([P, 2 * PASS], BF16, name="x_grouped%d" % k, tag=slot, align_bytes=64)
+            words = grouped[:, : count * PASS].bitcast(F32).rearrange("p (s c u) -> p s c u", c=P, u=2)
+            turn_and_weave(rounded, count, words, nc.scalar.copy if last else nc.scalar.copy)
+            waiting.append((j, group, grouped))
+            if k in (5, 7, 9):
+                store((5, 7, 9).index(k))
+        for job in waiting[len(pieces) - LAG - 1 :]:
+            multiply(*job)
+        store(x_blocks - 1)

@@ -20,7 +20,7 @@ PASS = 512
 PASSES = E // PASS
 N_TILE = 512
 SPARE = 16
-FIRST_CUTS = (0, 512, 1024, 2048)
+FIRST_CUTS = (0, 256, 1024, 2048)
 LAG = 3
 
 
@@ -44,10 +44,8 @@ def tile_attend_gmw_kernel(tc, xT, dyT, sw, tw, offs, offs2, out):
 
         src = keep.tile([P, E // 16], U16, name="src")
         dst = keep.tile([P, E // 16], U16, name="dst")
-        x_win = [window_tile(2 * PASS, "x_win%d" % j) for j in range(x_blocks)]
-        dy_win = [
-            window_tile(max(b - a for a, b in zip(cuts, cuts[1:])), "dy_win%d" % j) for j, cuts in enumerate(dy_cuts)
-        ]
+        x_win = [window_tile(2 * PASS, "x_win%d" % j) for j in range(2)]
+        dy_win = [window_tile(E, "dy_win%d" % j) for j in range(2)]
         tw_all = keep.tile([P, E], F32, name="tw_all")
         sw_all = keep.tile([P, E], F32, name="sw_all")
         ident = keep.tile([P, P], F32, name="ident")
@@ -56,16 +54,15 @@ def tile_attend_gmw_kernel(tc, xT, dyT, sw, tw, offs, offs2, out):
         nc.sync.dma_start(dy_win[0][:, :V], dyT[0:P, :])
         for a, b in zip(FIRST_CUTS, FIRST_CUTS[1:]):
             nc.sync.dma_start(tw_all[:, a:b], tw[:, a:b])
-        for j in range(1, dy_blocks):
-            nc.sync.dma_start(dy_win[j][:, :V], dyT[j * P : (j + 1) * P, :])
+        nc.sync.dma_start(dy_win[1][:, :V], dyT[P : 2 * P, :])
         nc.sync.dma_start(src[:], offs)
         nc.sync.dma_start(sw_all[:], sw)
-        for j in range(x_blocks):
+        for j in range(2):
             nc.sync.dma_start(x_win[j][:, :V], xT[j * P : (j + 1) * P, :])
-        for n, window in enumerate(dy_win + x_win):
-            nc.gpsimd.memset(window[:, V:], 0.0)
-            if n == 1:
-                make_identity(nc, ident[:])
+        for window in dy_win[:1] + x_win:
+            nc.vector.memset(window[:, V:], 0.0)
+        nc.gpsimd.memset(dy_win[1][:, V:], 0.0)
+        make_identity(nc, ident[:])
 
         def gather(picked, window, offsets, weights, a, b):
             nc.vector.tensor_tensor(picked, window[:].indirect(offsets[:, a // 16 : b // 16]), weights[:, a:b], MULT)
@@ -84,7 +81,10 @@ def tile_attend_gmw_kernel(tc, xT, dyT, sw, tw, offs, offs2, out):
             words = rounded[:].bitcast(F32)
             for n in range(2 * count):
                 nc.tensor.transpose(bank[:, n, :], words[:, n * P : (n + 1) * P], ident[:])
-            weave_copy(target, bank[:, : 2 * count, :].rearrange("p (s u) c -> p s c u", u=2))
+            weave_copy(
+                target.rearrange("p s (c i) u -> p s c u i", i=2),
+                bank[:, : 2 * count, :].rearrange("p (s u) (c i) -> p s c u i", u=2, i=2),
+            )
 
         dy_codes = [keep.tile([P, PASSES * N_TILE], U32, name="dy_codes%d" % h, align_bytes=64) for h in range(halves)]
         dy_scales = [keep.tile([P, PASSES * N_TILE], U8, name="dy_scales%d" % h, align_bytes=64) for h in range(halves)]
@@ -111,7 +111,9 @@ def tile_attend_gmw_kernel(tc, xT, dyT, sw, tw, offs, offs2, out):
             words = dy_grouped[h][:].bitcast(F32).rearrange("p (g j c u) -> p j g c u", g=PASSES, j=per_half, u=2)
             cuts = dy_cuts[block]
             for a, b in zip(cuts, cuts[1:]):
-                gather(picked[:, a:b], dy_win[block], dst, tw_all, a, b)
+                gather(picked[:, a:b], dy_win[block % 2], dst, tw_all, a, b)
+            if block + 2 < dy_blocks:
+                nc.sync.dma_start(dy_win[block % 2][:, :V], dyT[(block + 2) * P : (block + 3) * P, :])
             for g in (0, 2):
                 rounded = round_once(picked[:, g * PASS : (g + 2) * PASS], nc.scalar.copy)
                 turn_and_weave(rounded, 2, words[:, j, g : g + 2], nc.scalar.copy)
@@ -142,11 +144,13 @@ def tile_attend_gmw_kernel(tc, xT, dyT, sw, tw, offs, offs2, out):
                 result = ring.tile([P, N_TILE], F32, name="result", bufs=4)
                 rows = out[j * P : (j + 1) * P, h * N_TILE : (h + 1) * N_TILE]
                 if j == x_blocks - 1:
-                    if h == 0:
-                        nc.vector.tensor_copy(result[:], acc[j][h][:])
-                    else:
-                        nc.scalar.copy(result[:], acc[j][h][:])
-                    nc.sync.dma_start(rows, result[:])
+                    for part in range(2):
+                        cols = slice(part * N_TILE // 2, (part + 1) * N_TILE // 2)
+                        if h == 0:
+                            nc.vector.tensor_copy(result[:, cols], acc[j][h][:, cols])
+                        else:
+                            nc.scalar.copy(result[:, cols], acc[j][h][:, cols])
+                        nc.sync.dma_start(rows[:, cols], result[:, cols])
                 else:
                     nc.scalar.copy(result[:], acc[j][h][:])
                     nc.sync.dma_start(rows, result[:])
@@ -165,7 +169,9 @@ def tile_attend_gmw_kernel(tc, xT, dyT, sw, tw, offs, offs2, out):
                 picked = keep.tile([P, 2 * PASS], F32, name="x_picked%d" % k, tag="piece%d" % (k - LAG - 1), align_bytes=64)
             else:
                 picked = ring.tile([P, E], F32, name="picked", bufs=2)
-            gather(picked[:, : count * PASS], x_win[j], src, sw_all, group[0] * PASS, (group[-1] + 1) * PASS)
+            gather(picked[:, : count * PASS], x_win[j % 2], src, sw_all, group[0] * PASS, (group[-1] + 1) * PASS)
+            if group[-1] == PASSES - 1 and j + 2 < x_blocks:
+                nc.sync.dma_start(x_win[j % 2][:, :V], xT[(j + 2) * P : (j + 3) * P, :])
             last = k == len(pieces) - 1
             rounded = round_once(picked[:, : count * PASS], nc.vector.tensor_copy if last else nc.scalar.copy)
             grouped = keep.tile([P, 2 * PASS], BF16, name="x_grouped%d" % k, tag=slot, align_bytes=64)

@@ -8,178 +8,208 @@ FLOPS = 2 * E * D * DV
 
 F32 = mybir.dt.float32
 BF16 = mybir.dt.bfloat16
+I32 = mybir.dt.int32
 U32 = mybir.dt.uint32
 U16 = mybir.dt.uint16
 U8 = mybir.dt.uint8
 E4M3 = mybir.dt.float8_e4m3fn_x4
 E5M2 = mybir.dt.float8_e5m2_x4
 MULT = mybir.AluOpType.mult
+COPY = mybir.ActivationFunctionType.Copy
 
 P = 128
 PASS = 512
 PASSES = E // PASS
-N_TILE = 512
-SPARE = 16
-FIRST_CUTS = (0, 256, 1024, 2048)
-LAG = 3
+PIECE = 2 * PASS
+SCALAR_WINDOW = PIECE + 16
+VECTOR_WINDOW = 1376
+X_BLOCKS = D // P
+DY_BLOCKS = DV // P
 
 
 def tile_attend_gmw_kernel(tc, xT, dyT, sw, tw, offs, offs2, out):
     nc = tc.nc
-    x_blocks = D // P
-    dy_blocks = DV // P
-    halves = DV // N_TILE
-    per_half = N_TILE // P
+    scalar_blocks = [("x", j) for j in range(3)] + [("dy", m) for m in range(5)]
+    vector_blocks = [("x", 3)] + [("dy", m) for m in range(5, 8)]
+    table = {"x": xT, "dy": dyT}
 
     with ExitStack() as ctx:
         keep = ctx.enter_context(tc.tile_pool(name="keep", bufs=1))
         ring = ctx.enter_context(tc.tile_pool(name="ring", bufs=3))
-        turn = ctx.enter_context(tc.psum_pool(name="turn", bufs=2))
-        sums = ctx.enter_context(tc.psum_pool(name="sums", bufs=3))
+        psum = ctx.enter_context(tc.psum_pool(name="psum", bufs=2))
 
-        dy_cuts = [FIRST_CUTS] + [(0, 2048)] * (dy_blocks - 1)
-
-        def window_tile(longest, name):
-            return keep.tile([P, max(V, longest) + SPARE], F32, name=name)
-
-        src = keep.tile([P, E // 16], U16, name="src")
-        dst = keep.tile([P, E // 16], U16, name="dst")
-        x_win = [window_tile(2 * PASS, "x_win%d" % j) for j in range(2)]
-        dy_win = [window_tile(E, "dy_win%d" % j) for j in range(2)]
-        tw_all = keep.tile([P, E], F32, name="tw_all")
-        sw_all = keep.tile([P, E], F32, name="sw_all")
+        lists = {name: keep.tile([P, E // 16], U16, name="list_" + name) for name in ("x", "dy")}
+        rows = {name: [keep.tile([P, PIECE], F32, name="rows_%s%d" % (name, h)) for h in range(2)] for name in ("x", "dy")}
+        columns = {name: keep.tile([P, PASSES, 4], F32, name="columns_" + name) for name in ("x", "dy")}
+        s_win = {name: [keep.tile([P, SCALAR_WINDOW], F32, name="s_win_%s%d" % (name, i)) for i in range(2)] for name in ("x", "dy")}
+        v_win = {
+            "x": [keep.tile([P, VECTOR_WINDOW], F32, name="v_win_x")],
+            "dy": [keep.tile([P, VECTOR_WINDOW], F32, name="v_win_dy%d" % i) for i in range(2)],
+        }
         ident = keep.tile([P, P], F32, name="ident")
 
-        nc.sync.dma_start(dst[:], offs2)
-        nc.sync.dma_start(dy_win[0][:, :V], dyT[0:P, :])
-        for a, b in zip(FIRST_CUTS, FIRST_CUTS[1:]):
-            nc.sync.dma_start(tw_all[:, a:b], tw[:, a:b])
-        nc.sync.dma_start(dy_win[1][:, :V], dyT[P : 2 * P, :])
-        nc.sync.dma_start(src[:], offs)
-        nc.sync.dma_start(sw_all[:], sw)
-        for j in range(2):
-            nc.sync.dma_start(x_win[j][:, :V], xT[j * P : (j + 1) * P, :])
-        for window in dy_win[:1] + x_win:
-            nc.vector.memset(window[:, V:], 0.0)
-        nc.gpsimd.memset(dy_win[1][:, V:], 0.0)
+        def s_window(s):
+            name, block = scalar_blocks[s]
+            return s_win[name][block % 2]
+
+        def v_window(v):
+            name, block = vector_blocks[v]
+            return v_win[name][(v - 1) % len(v_win[name])]
+
+        def load_block(window, name, block):
+            nc.sync.dma_start(window[:, :V], table[name][block * P : (block + 1) * P, :])
+
+        def load_columns(name, weights):
+            nc.sync.dma_start(columns[name][:], weights[0:1, :].rearrange("o (g p t) -> p (o g) t", p=P, t=4))
+
+        nc.sync.dma_start(lists["x"][:], offs)
+        load_block(s_window(0), *scalar_blocks[0])
+        load_block(v_window(0), *vector_blocks[0])
+        load_columns("x", sw)
+        nc.sync.dma_start(rows["x"][0][:], sw[:, :PIECE])
+        load_block(s_window(1), *scalar_blocks[1])
+        nc.sync.dma_start(rows["x"][1][:], sw[:, PIECE:])
+        nc.sync.dma_start(lists["dy"][:], offs2)
+        load_block(v_window(1), *vector_blocks[1])
+        load_columns("dy", tw)
+        load_block(s_window(3), *scalar_blocks[3])
+        nc.sync.dma_start(rows["dy"][0][:], tw[:, :PIECE])
+        nc.sync.dma_start(rows["dy"][1][:], tw[:, PIECE:])
+        load_block(s_window(4), *scalar_blocks[4])
+        load_block(v_window(2), *vector_blocks[2])
+
+        for window in s_win["x"][:1] + v_win["x"] + s_win["x"][1:] + v_win["dy"]:
+            nc.vector.memset(window[:, V:].bitcast(I32), 0)
         make_identity(nc, ident[:])
+        for window in s_win["dy"]:
+            nc.gpsimd.memset(window[:, V:].bitcast(I32), 0)
 
-        def gather(picked, window, offsets, weights, a, b):
-            nc.vector.tensor_tensor(picked, window[:].indirect(offsets[:, a // 16 : b // 16]), weights[:, a:b], MULT)
+        s_picked, s_bank, s_grouped = {}, {}, {}
+        v_banks, v_grouped = {}, {}
+        x_codes, x_scales = {}, {}
+        pending = []
 
-        def round_once(picked, round_copy):
-            count = picked.shape[1] // PASS
-            rounded = ring.tile([P, 2 * PASS], BF16, name="rounded")
-            round_copy(
-                rounded[:, : count * PASS].rearrange("f (g u q r) -> f g u q r", g=count, u=2, r=16),
-                picked.rearrange("f (g q u r) -> f g u q r", g=count, u=2, r=16),
-            )
-            return rounded
+        def offsets(name, half):
+            return lists[name][:, half * PIECE // 16 : (half + 1) * PIECE // 16]
 
-        def turn_and_weave(rounded, count, target, weave_copy):
-            bank = turn.tile([P, 4, P], F32, name="bank")
+        def scalar_gather(k):
+            s, half = divmod(k, 2)
+            name, block = scalar_blocks[s]
+            s_picked[k] = ring.tile([P, PIECE], F32, name="s_picked")
+            nc.scalar.activation(s_picked[k][:], s_window(s)[:].indirect(offsets(name, half)), COPY)
+            if half == 1 and s + 2 < len(scalar_blocks) and scalar_blocks[s + 2][0] == name:
+                load_block(s_window(s), *scalar_blocks[s + 2])
+
+        def multiply_and_turn(k):
+            s, half = divmod(k, 2)
+            rounded = ring.tile([P, PIECE], BF16, name="rounded")
+            nc.vector.tensor_tensor(rounded[:], s_picked[k][:], rows[scalar_blocks[s][0]][half][:], MULT)
             words = rounded[:].bitcast(F32)
-            for n in range(2 * count):
-                nc.tensor.transpose(bank[:, n, :], words[:, n * P : (n + 1) * P], ident[:])
-            weave_copy(
-                target.rearrange("p s (c i) u -> p s c u i", i=2),
-                bank[:, : 2 * count, :].rearrange("p (s u) (c i) -> p s c u i", u=2, i=2),
+            s_bank[k] = psum.tile([P, 2, 2, P], F32, name="s_bank")
+            for g in range(2):
+                for u in range(2):
+                    nc.tensor.transpose(s_bank[k][:, g, u, :], words[:, 2 * P * g + u : 2 * P * (g + 1) : 2], ident[:])
+
+        def weave(k):
+            s, half = divmod(k, 2)
+            if half == 0:
+                s_grouped[s] = ring.tile([P, E], BF16, name="s_grouped", align_bytes=64)
+            target = s_grouped[s][:, half * PIECE : (half + 1) * PIECE].bitcast(F32)
+            nc.scalar.copy(
+                target.rearrange("p (g c i u) -> p g c u i", g=2, i=2, u=2),
+                s_bank[k][:].rearrange("p g u (c i) -> p g c u i", i=2),
             )
 
-        dy_codes = [keep.tile([P, PASSES * N_TILE], U32, name="dy_codes%d" % h, align_bytes=64) for h in range(halves)]
-        dy_scales = [keep.tile([P, PASSES * N_TILE], U8, name="dy_scales%d" % h, align_bytes=64) for h in range(halves)]
+        def vector_gather_and_turn(r):
+            v, half = divmod(r, 2)
+            name, block = vector_blocks[v]
+            picked = ring.tile([P, PIECE], F32, name="v_picked", bufs=2)
+            nc.vector.tensor_copy(
+                picked[:].bitcast(U32).rearrange("f (u s w) -> f s u w", u=2, w=2),
+                v_window(v)[:].bitcast(U32).indirect(offsets(name, half)),
+            )
+            if half == 1 and v >= 1 and v + 2 < len(vector_blocks):
+                load_block(v_window(v), *vector_blocks[v + 2])
+            v_banks[r] = []
+            for g in range(2):
+                bank = psum.tile([P, 4, P], F32, name="v_bank", bufs=4)
+                v_banks[r].append(bank)
+                for u in range(2):
+                    for w in range(2):
+                        start = u * PASS + g * 2 * P
+                        nc.tensor.transpose(bank[:, 2 * u + w, :], picked[:, start + w : start + 2 * P : 2], ident[:])
 
-        def quantise_half(h, grouped):
-            width = 1024
-            for a in range(0, PASSES * N_TILE, width):
-                nc.vector.quantize_mx(
-                    out=dy_codes[h][:, a : a + width].bitcast(E5M2),
-                    scales=dy_scales[h][:, a : a + width],
-                    in_=grouped[:, 4 * a : 4 * (a + width)],
+        def multiply_out(r):
+            v, half = divmod(r, 2)
+            if half == 0:
+                v_grouped[v] = ring.tile([P, E], BF16, name="v_grouped", bufs=2, align_bytes=64)
+            for g in range(2):
+                a = (2 * half + g) * PASS
+                nc.vector.tensor_tensor(
+                    v_grouped[v][:, a : a + PASS].rearrange("p (c t) -> p c t", t=4),
+                    v_banks[r][g][:].rearrange("p t c -> p c t"),
+                    columns[vector_blocks[v][0]][:, 2 * half + g : 2 * half + g + 1, :].to_broadcast([P, P, 4]),
+                    MULT,
                 )
 
-        dy_grouped = []
-        for block in range(dy_blocks):
-            h, j = divmod(block, per_half)
-            if block == per_half + 2:
-                quantise_half(0, dy_grouped[0])
-            picked = ring.tile([P, E], F32, name="picked", bufs=2)
-            if j == 0:
-                dy_grouped.append(
-                    keep.tile([P, PASSES * 4 * N_TILE], BF16, name="dy_grouped%d" % h, tag="half%d" % h, align_bytes=64)
-                )
-            words = dy_grouped[h][:].bitcast(F32).rearrange("p (g j c u) -> p j g c u", g=PASSES, j=per_half, u=2)
-            cuts = dy_cuts[block]
-            for a, b in zip(cuts, cuts[1:]):
-                gather(picked[:, a:b], dy_win[block % 2], dst, tw_all, a, b)
-            if block + 2 < dy_blocks:
-                nc.sync.dma_start(dy_win[block % 2][:, :V], dyT[(block + 2) * P : (block + 3) * P, :])
-            for g in (0, 2):
-                rounded = round_once(picked[:, g * PASS : (g + 2) * PASS], nc.scalar.copy)
-                turn_and_weave(rounded, 2, words[:, j, g : g + 2], nc.scalar.copy)
+        waiting = []
 
-        acc = {}
+        def quantise(name, block, grouped):
+            if name == "x":
+                x_codes[block] = keep.tile([P, PASSES * P], U32, name="x_codes%d" % block, align_bytes=64)
+                x_scales[block] = keep.tile([P, PASSES * P], U8, name="x_scales%d" % block, align_bytes=64)
+                nc.vector.quantize_mx(out=x_codes[block][:].bitcast(E4M3), scales=x_scales[block][:], in_=grouped[:])
+            else:
+                codes = ring.tile([P, PASSES * P], U32, name="dy_codes", align_bytes=64)
+                scales = ring.tile([P, PASSES * P], U8, name="dy_scales", align_bytes=64)
+                nc.vector.quantize_mx(out=codes[:].bitcast(E5M2), scales=scales[:], in_=grouped[:])
+                waiting.append((block, codes, scales))
+            if len(x_codes) == X_BLOCKS:
+                for job in waiting:
+                    product(*job)
+                waiting.clear()
 
-        def multiply(j, group, grouped):
-            width = len(group) * P
-            codes = ring.tile([P, 2 * P], U32, name="x_codes", align_bytes=64)
-            scales = ring.tile([P, 2 * P], U8, name="x_scales", align_bytes=64)
-            nc.vector.quantize_mx(out=codes[:, :width].bitcast(E4M3), scales=scales[:, :width], in_=grouped[:, : 4 * width])
-            if group[0] == 0:
-                acc[j] = [sums.tile([P, N_TILE], F32, name="acc%d" % h) for h in range(halves)]
-            for i, g in enumerate(group):
-                for h in range(halves):
+        def product(block, codes, scales):
+            acc = psum.tile([P, X_BLOCKS, P], F32, name="acc")
+            for j in range(X_BLOCKS):
+                for g in range(PASSES):
+                    cols = slice(g * P, (g + 1) * P)
                     nc.tensor.matmul_mx(
-                        out=acc[j][h][:],
-                        lhsT=codes[:, i * P : (i + 1) * P].bitcast(E4M3),
-                        lhsT_scale=scales[:, i * P : (i + 1) * P],
-                        rhs=dy_codes[h][:, g * N_TILE : (g + 1) * N_TILE].bitcast(E5M2),
-                        rhs_scale=dy_scales[h][:, g * N_TILE : (g + 1) * N_TILE],
+                        out=acc[:, j, :],
+                        lhsT=x_codes[j][:, cols].bitcast(E4M3),
+                        lhsT_scale=x_scales[j][:, cols],
+                        rhs=codes[:, cols].bitcast(E5M2),
+                        rhs_scale=scales[:, cols],
                         start=(g == 0),
                         stop=(g == PASSES - 1),
                     )
+            pending.append((block, acc))
 
-        def store(j):
-            for h in range(halves):
-                result = ring.tile([P, N_TILE], F32, name="result", bufs=4)
-                rows = out[j * P : (j + 1) * P, h * N_TILE : (h + 1) * N_TILE]
-                if j == x_blocks - 1:
-                    for part in range(2):
-                        cols = slice(part * N_TILE // 2, (part + 1) * N_TILE // 2)
-                        if h == 0:
-                            nc.vector.tensor_copy(result[:, cols], acc[j][h][:, cols])
-                        else:
-                            nc.scalar.copy(result[:, cols], acc[j][h][:, cols])
-                        nc.sync.dma_start(rows[:, cols], result[:, cols])
-                else:
-                    nc.scalar.copy(result[:], acc[j][h][:])
-                    nc.sync.dma_start(rows, result[:])
+        def store_pending():
+            for block, acc in pending:
+                result = ring.tile([P, X_BLOCKS, P], F32, name="result")
+                nc.scalar.copy(result[:], acc[:])
+                nc.sync.dma_start(out[:, block * P : (block + 1) * P].rearrange("(j p) c -> p j c", p=P), result[:])
+            pending.clear()
 
-        pieces = [(j, group) for j in range(x_blocks - 1) for group in ((0, 1), (2, 3))]
-        pieces = pieces + [(x_blocks - 1, group) for group in ((0,), (1,), (2,), (3,))]
-        waiting = []
-        for k, (j, group) in enumerate(pieces):
-            slot = "piece%d" % k
-            if k == 3:
-                quantise_half(1, dy_grouped[1])
-            if k > LAG:
-                multiply(*waiting[k - LAG - 1])
-            count = len(group)
-            if k in ():
-                picked = keep.tile([P, 2 * PASS], F32, name="x_picked%d" % k, tag="piece%d" % (k - LAG - 1), align_bytes=64)
-            else:
-                picked = ring.tile([P, E], F32, name="picked", bufs=2)
-            gather(picked[:, : count * PASS], x_win[j % 2], src, sw_all, group[0] * PASS, (group[-1] + 1) * PASS)
-            if group[-1] == PASSES - 1 and j + 2 < x_blocks:
-                nc.sync.dma_start(x_win[j % 2][:, :V], xT[(j + 2) * P : (j + 3) * P, :])
-            last = k == len(pieces) - 1
-            rounded = round_once(picked[:, : count * PASS], nc.vector.tensor_copy if last else nc.scalar.copy)
-            grouped = keep.tile([P, 2 * PASS], BF16, name="x_grouped%d" % k, tag=slot, align_bytes=64)
-            words = grouped[:, : count * PASS].bitcast(F32).rearrange("p (s c u) -> p s c u", c=P, u=2)
-            turn_and_weave(rounded, count, words, nc.scalar.copy if last else nc.scalar.copy)
-            waiting.append((j, group, grouped))
-            if k in (5, 7, 9):
-                store((5, 7, 9).index(k))
-        for job in waiting[len(pieces) - LAG - 1 :]:
-            multiply(*job)
-        store(x_blocks - 1)
+        rounds = len(scalar_blocks)
+        for r in range(rounds + 2):
+            if r < rounds:
+                scalar_gather(2 * r)
+                vector_gather_and_turn(r)
+            if 1 <= r <= rounds:
+                weave(2 * r - 2)
+            if r >= 2:
+                quantise(*scalar_blocks[r - 2], s_grouped[r - 2])
+            if 1 <= r <= rounds:
+                multiply_and_turn(2 * r - 1)
+            if r < rounds:
+                scalar_gather(2 * r + 1)
+                multiply_out(r)
+            if 1 <= r <= rounds:
+                weave(2 * r - 1)
+            if r < rounds:
+                multiply_and_turn(2 * r)
+            store_pending()
+            if r < rounds and r % 2 == 1:
+                quantise(*vector_blocks[r // 2], v_grouped[r // 2])

@@ -23,6 +23,7 @@ PASSES = E // PASS
 PIECE = 2 * PASS
 SCALAR_WINDOW = PIECE + 16
 VECTOR_WINDOW = 1376
+TURN_BANKS = 6
 X_BLOCKS = D // P
 DY_BLOCKS = DV // P
 
@@ -78,11 +79,18 @@ def tile_attend_gmw_kernel(tc, xT, dyT, sw, tw, offs, offs2, out):
         load_block(s_window(4), *scalar_blocks[4])
         load_block(v_window(2), *vector_blocks[2])
 
-        for window in s_win["x"][:1] + v_win["x"] + s_win["x"][1:] + v_win["dy"]:
+        for window in s_win["x"][:1] + v_win["x"] + s_win["x"][1:]:
             nc.vector.memset(window[:, V:].bitcast(I32), 0)
         make_identity(nc, ident[:])
-        for window in s_win["dy"]:
+        for window in v_win["dy"][:1] + s_win["dy"] + v_win["dy"][1:]:
             nc.gpsimd.memset(window[:, V:].bitcast(I32), 0)
+
+        banks = [psum.tile([P, 4, P], F32, name="bank%d" % i, bufs=1) for i in range(TURN_BANKS)]
+        taken = []
+
+        def next_bank():
+            taken.append(len(taken))
+            return banks[taken[-1] % TURN_BANKS]
 
         s_picked, s_bank, s_grouped = {}, {}, {}
         v_banks, v_grouped = {}, {}
@@ -103,21 +111,21 @@ def tile_attend_gmw_kernel(tc, xT, dyT, sw, tw, offs, offs2, out):
         def multiply_and_turn(k):
             s, half = divmod(k, 2)
             rounded = ring.tile([P, PIECE], BF16, name="rounded")
-            nc.vector.tensor_tensor(rounded[:], s_picked[k][:], rows[scalar_blocks[s][0]][half][:], MULT)
+            nc.gpsimd.tensor_tensor(rounded[:], s_picked[k][:], rows[scalar_blocks[s][0]][half][:], MULT)
             words = rounded[:].bitcast(F32)
-            s_bank[k] = psum.tile([P, 2, 2, P], F32, name="s_bank")
+            s_bank[k] = next_bank()
             for g in range(2):
                 for u in range(2):
-                    nc.tensor.transpose(s_bank[k][:, g, u, :], words[:, 2 * P * g + u : 2 * P * (g + 1) : 2], ident[:])
+                    nc.tensor.transpose(s_bank[k][:, 2 * g + u, :], words[:, 2 * P * g + u : 2 * P * (g + 1) : 2], ident[:])
 
         def weave(k):
             s, half = divmod(k, 2)
             if half == 0:
                 s_grouped[s] = ring.tile([P, E], BF16, name="s_grouped", align_bytes=64)
             target = s_grouped[s][:, half * PIECE : (half + 1) * PIECE].bitcast(F32)
-            nc.scalar.copy(
+            nc.vector.tensor_copy(
                 target.rearrange("p (g c i u) -> p g c u i", g=2, i=2, u=2),
-                s_bank[k][:].rearrange("p g u (c i) -> p g c u i", i=2),
+                s_bank[k][:].rearrange("p (g u) (c i) -> p g c u i", u=2, i=2),
             )
 
         def vector_gather_and_turn(r):
@@ -132,7 +140,7 @@ def tile_attend_gmw_kernel(tc, xT, dyT, sw, tw, offs, offs2, out):
                 load_block(v_window(v), *vector_blocks[v + 2])
             v_banks[r] = []
             for g in range(2):
-                bank = psum.tile([P, 4, P], F32, name="v_bank", bufs=4)
+                bank = next_bank()
                 v_banks[r].append(bank)
                 for u in range(2):
                     for w in range(2):
@@ -198,18 +206,17 @@ def tile_attend_gmw_kernel(tc, xT, dyT, sw, tw, offs, offs2, out):
                 scalar_gather(2 * r)
                 vector_gather_and_turn(r)
             if 1 <= r <= rounds:
-                weave(2 * r - 2)
-            if r >= 2:
-                quantise(*scalar_blocks[r - 2], s_grouped[r - 2])
-            if 1 <= r <= rounds:
                 multiply_and_turn(2 * r - 1)
+                weave(2 * r - 2)
             if r < rounds:
                 scalar_gather(2 * r + 1)
                 multiply_out(r)
             if 1 <= r <= rounds:
                 weave(2 * r - 1)
+            if r < rounds and r % 2 == 1:
+                quantise(*vector_blocks[r // 2], v_grouped[r // 2])
             if r < rounds:
                 multiply_and_turn(2 * r)
             store_pending()
-            if r < rounds and r % 2 == 1:
-                quantise(*vector_blocks[r // 2], v_grouped[r // 2])
+            if 1 <= r <= rounds:
+                quantise(*scalar_blocks[r - 1], s_grouped[r - 1])

@@ -20,203 +20,265 @@ COPY = mybir.ActivationFunctionType.Copy
 P = 128
 PASS = 512
 PASSES = E // PASS
-PIECE = 2 * PASS
-SCALAR_WINDOW = PIECE + 16
-VECTOR_WINDOW = 1376
-TURN_BANKS = 6
+WINDOW = 704
 X_BLOCKS = D // P
 DY_BLOCKS = DV // P
+N_TILE = 256
+QUARTERS = DV // N_TILE
+SUM_BANKS = 4
+TURN_BANKS = 4
+PICKED = 3
+THREE = (3, 6, 9)
+DEALT = 3
+LATE = 3
+FIRST_BATCH = 4
+DY_BATCH = 2
+X_BATCH = 4
+ROADS = ["FFBC" if b in THREE else "FFCC" for b in range(12)]
+ORDER = ["x", "dy", "dy"] * 4
+WARM = 1
 
 
 def tile_attend_gmw_kernel(tc, xT, dyT, sw, tw, offs, offs2, out):
     nc = tc.nc
-    scalar_blocks = [("x", j) for j in range(3)] + [("dy", m) for m in range(5)]
-    vector_blocks = [("x", 3)] + [("dy", m) for m in range(5, 8)]
+    blocks = [(name, ORDER[:b].count(name)) for b, name in enumerate(ORDER)]
     table = {"x": xT, "dy": dyT}
+    weights = {"x": sw, "dy": tw}
+    last = len(blocks) - 1
 
     with ExitStack() as ctx:
         keep = ctx.enter_context(tc.tile_pool(name="keep", bufs=1))
         ring = ctx.enter_context(tc.tile_pool(name="ring", bufs=3))
-        psum = ctx.enter_context(tc.psum_pool(name="psum", bufs=2))
+        psum = ctx.enter_context(tc.psum_pool(name="psum", bufs=1))
 
         lists = {name: keep.tile([P, E // 16], U16, name="list_" + name) for name in ("x", "dy")}
-        rows = {name: [keep.tile([P, PIECE], F32, name="rows_%s%d" % (name, h)) for h in range(2)] for name in ("x", "dy")}
-        columns = {name: keep.tile([P, PASSES, 4], F32, name="columns_" + name) for name in ("x", "dy")}
-        s_win = {name: [keep.tile([P, SCALAR_WINDOW], F32, name="s_win_%s%d" % (name, i)) for i in range(2)] for name in ("x", "dy")}
-        v_win = {
-            "x": [keep.tile([P, VECTOR_WINDOW], F32, name="v_win_x")],
-            "dy": [keep.tile([P, VECTOR_WINDOW], F32, name="v_win_dy%d" % i) for i in range(2)],
+        rows = {
+            (name, g): keep.tile([P, PASS], F32, name="rows_%s%d" % (name, g))
+            for name in ("dy", "x")
+            for g in range(PASSES)
+            if any(ROADS[b][g] in "EF" and ORDER[b] == name for b in range(len(ORDER)))
         }
+        columns = {name: keep.tile([P, PASSES, 4], F32, name="columns_" + name) for name in ("x", "dy")}
+        windows = [keep.tile([P, WINDOW], F32, name="window%d" % b) for b in range(len(blocks))]
         ident = keep.tile([P, P], F32, name="ident")
+        banks = [psum.tile([P, 4, P], F32, name="bank%d" % i) for i in range(PASSES + SUM_BANKS)]
 
-        def s_window(s):
-            name, block = scalar_blocks[s]
-            return s_win[name][block % 2]
+        def load_block(b):
+            name, block = blocks[b]
+            nc.sync.dma_start(windows[b][:, :V], table[name][block * P : (block + 1) * P, :])
 
-        def v_window(v):
-            name, block = vector_blocks[v]
-            return v_win[name][(v - 1) % len(v_win[name])]
+        def load_columns(name):
+            nc.sync.dma_start(columns[name][:], weights[name][0:1, :].rearrange("o (g p t) -> p (o g) t", p=P, t=4))
 
-        def load_block(window, name, block):
-            nc.sync.dma_start(window[:, :V], table[name][block * P : (block + 1) * P, :])
-
-        def load_columns(name, weights):
-            nc.sync.dma_start(columns[name][:], weights[0:1, :].rearrange("o (g p t) -> p (o g) t", p=P, t=4))
+        def load_rows(name, g):
+            nc.sync.dma_start(rows[name, g][:], weights[name][:, g * PASS : (g + 1) * PASS])
 
         nc.sync.dma_start(lists["x"][:], offs)
-        load_block(s_window(0), *scalar_blocks[0])
-        load_block(v_window(0), *vector_blocks[0])
-        load_columns("x", sw)
-        nc.sync.dma_start(rows["x"][0][:], sw[:, :PIECE])
-        load_block(s_window(1), *scalar_blocks[1])
-        nc.sync.dma_start(rows["x"][1][:], sw[:, PIECE:])
+        load_block(0)
+        load_rows("x", 0)
+        load_columns("x")
+        load_rows("x", 1)
         nc.sync.dma_start(lists["dy"][:], offs2)
-        load_block(v_window(1), *vector_blocks[1])
-        load_columns("dy", tw)
-        load_block(s_window(3), *scalar_blocks[3])
-        nc.sync.dma_start(rows["dy"][0][:], tw[:, :PIECE])
-        nc.sync.dma_start(rows["dy"][1][:], tw[:, PIECE:])
-        load_block(s_window(4), *scalar_blocks[4])
-        load_block(v_window(2), *vector_blocks[2])
+        load_block(1)
+        load_rows("dy", 0)
+        load_columns("dy")
+        load_rows("dy", 1)
+        for b in range(2, len(blocks)):
+            load_block(b)
 
-        for window in s_win["x"][:1] + v_win["x"] + s_win["x"][1:]:
+        for window in windows:
             nc.vector.memset(window[:, V:].bitcast(I32), 0)
         make_identity(nc, ident[:])
-        for window in v_win["dy"][:1] + s_win["dy"] + v_win["dy"][1:]:
-            nc.gpsimd.memset(window[:, V:].bitcast(I32), 0)
+        if WARM:
+            warm = keep.tile([P, 1], F32, name="warm")
+            nc.scalar.activation(warm[:], windows[0][:, V : V + 1], COPY)
 
-        banks = [psum.tile([P, 4, P], F32, name="bank%d" % i, bufs=1) for i in range(TURN_BANKS)]
-        taken = []
+        dy_grouped = [keep.tile([P, 2 * PASSES * PASS], BF16, name="dy_grouped%d" % q, align_bytes=64) for q in range(QUARTERS)]
+        dy_codes = [keep.tile([P, PASSES * N_TILE], U32, name="dy_codes%d" % q, align_bytes=64) for q in range(QUARTERS)]
+        dy_scales = [keep.tile([P, PASSES * N_TILE], U8, name="dy_scales%d" % q, align_bytes=64) for q in range(QUARTERS)]
+        x_grouped = [keep.tile([P, PASSES * PASS], BF16, name="x_grouped%d" % j, align_bytes=64) for j in range(X_BLOCKS)]
+        x_codes = [keep.tile([P, PASSES * P], U32, name="x_codes%d" % j, align_bytes=64) for j in range(X_BLOCKS)]
+        x_scales = [keep.tile([P, PASSES * P], U8, name="x_scales%d" % j, align_bytes=64) for j in range(X_BLOCKS)]
+        s_slots = [keep.tile([P, PASS], F32, name="s_slot%d" % i) for i in range(PICKED)]
+        v_slots = [keep.tile([P, PASS], F32, name="v_slot%d" % i) for i in range(DEALT)]
 
-        def next_bank():
-            taken.append(len(taken))
-            return banks[taken[-1] % TURN_BANKS]
+        def grouped(b):
+            name, block = blocks[b]
+            if name == "x":
+                return x_grouped[block][:].rearrange("p (g c) -> p g c", g=PASSES)
+            return dy_grouped[block // 2][:].rearrange("p (g m c) -> p g m c", g=PASSES, m=2)[:, :, block % 2, :]
 
-        s_picked, s_bank, s_grouped = {}, {}, {}
-        v_banks, v_grouped = {}, {}
-        x_codes, x_scales = {}, {}
-        pending = []
+        def offsets(b, g):
+            return lists[blocks[b][0]][:, g * PASS // 16 : (g + 1) * PASS // 16]
 
-        def offsets(name, half):
-            return lists[name][:, half * PIECE // 16 : (half + 1) * PIECE // 16]
+        picked, rounded, turned = {}, {}, {}
+        dealt_count, slot_count, turn_count, room_count = [], [], [], []
+        rooms = [keep.tile([P, PASS], BF16, name="room%d" % i)[:] for i in range(FIRST_BATCH)]
+        units = [(b, g) for b in range(len(blocks)) for g in range(2)]
 
-        def scalar_gather(k):
-            s, half = divmod(k, 2)
-            name, block = scalar_blocks[s]
-            s_picked[k] = ring.tile([P, PIECE], F32, name="s_picked")
-            nc.scalar.activation(s_picked[k][:], s_window(s)[:].indirect(offsets(name, half)), COPY)
-            if half == 1 and s + 2 < len(scalar_blocks) and scalar_blocks[s + 2][0] == name:
-                load_block(s_window(s), *scalar_blocks[s + 2])
+        def turn_bank():
+            turn_count.append(0)
+            return banks[len(turn_count) % TURN_BANKS]
 
-        def multiply_and_turn(k):
-            s, half = divmod(k, 2)
-            rounded = ring.tile([P, PIECE], BF16, name="rounded")
-            nc.gpsimd.tensor_tensor(rounded[:], s_picked[k][:], rows[scalar_blocks[s][0]][half][:], MULT)
-            words = rounded[:].bitcast(F32)
-            s_bank[k] = next_bank()
-            for g in range(2):
+        def scalar_gather(b, g):
+            picked[b, g] = s_slots[len(slot_count) % PICKED]
+            slot_count.append(0)
+            nc.scalar.activation(picked[b, g][:], windows[b][:].indirect(offsets(b, g)), COPY)
+
+        def scalar_lane():
+            while rooms and units:
+                b, g = units.pop(0)
+                scalar_gather(b, g)
+                rounded[b, g] = rooms.pop(0)
+                nc.gpsimd.tensor_tensor(rounded[b, g], picked[b, g][:], rows[blocks[b][0], g][:], MULT)
+
+        def gather_third(b):
+            picked[b, 2] = v_slots[len(dealt_count) % DEALT]
+            dealt_count.append(0)
+            nc.scalar.activation(picked[b, 2][:], windows[b][:].indirect(offsets(b, 2)), COPY)
+
+        def turn_and_weave(b, g, count):
+            bank = turn_bank()
+            for i in range(count):
+                words = rounded[b, g + i].bitcast(F32)
                 for u in range(2):
-                    nc.tensor.transpose(s_bank[k][:, 2 * g + u, :], words[:, 2 * P * g + u : 2 * P * (g + 1) : 2], ident[:])
-
-        def weave(k):
-            s, half = divmod(k, 2)
-            if half == 0:
-                s_grouped[s] = ring.tile([P, E], BF16, name="s_grouped", align_bytes=64)
-            target = s_grouped[s][:, half * PIECE : (half + 1) * PIECE].bitcast(F32)
-            nc.vector.tensor_copy(
-                target.rearrange("p (g c i u) -> p g c u i", g=2, i=2, u=2),
-                s_bank[k][:].rearrange("p (g u) (c i) -> p g c u i", u=2, i=2),
+                    nc.tensor.transpose(bank[:, 2 * i + u, :], words[:, u : 2 * P : 2], ident[:])
+            nc.scalar.copy(
+                grouped(b)[:, g : g + count, :].bitcast(F32).rearrange("p g (c i u) -> p g c u i", i=2, u=2),
+                bank[:, : 2 * count, :].rearrange("p (g u) (c i) -> p g c u i", u=2, i=2),
             )
 
-        def vector_gather_and_turn(r):
-            v, half = divmod(r, 2)
-            name, block = vector_blocks[v]
-            picked = ring.tile([P, PIECE], F32, name="v_picked", bufs=2)
+        def vector_gather_and_turn(b, g):
+            dealt = v_slots[len(dealt_count) % DEALT]
+            dealt_count.append(0)
             nc.vector.tensor_copy(
-                picked[:].bitcast(U32).rearrange("f (u s w) -> f s u w", u=2, w=2),
-                v_window(v)[:].bitcast(U32).indirect(offsets(name, half)),
+                dealt[:].bitcast(U32).rearrange("f (u s w) -> f s u w", u=2, w=2),
+                windows[b][:].bitcast(U32).indirect(offsets(b, g)),
             )
-            if half == 1 and v >= 1 and v + 2 < len(vector_blocks):
-                load_block(v_window(v), *vector_blocks[v + 2])
-            v_banks[r] = []
-            for g in range(2):
-                bank = next_bank()
-                v_banks[r].append(bank)
-                for u in range(2):
-                    for w in range(2):
-                        start = u * PASS + g * 2 * P
-                        nc.tensor.transpose(bank[:, 2 * u + w, :], picked[:, start + w : start + 2 * P : 2], ident[:])
+            turned[b, g] = turn_bank()
+            for u in range(2):
+                for w in range(2):
+                    nc.tensor.transpose(turned[b, g][:, 2 * u + w, :], dealt[:, 2 * P * u + w : 2 * P * (u + 1) : 2], ident[:])
 
-        def multiply_out(r):
-            v, half = divmod(r, 2)
-            if half == 0:
-                v_grouped[v] = ring.tile([P, E], BF16, name="v_grouped", bufs=2, align_bytes=64)
-            for g in range(2):
-                a = (2 * half + g) * PASS
-                nc.vector.tensor_tensor(
-                    v_grouped[v][:, a : a + PASS].rearrange("p (c t) -> p c t", t=4),
-                    v_banks[r][g][:].rearrange("p t c -> p c t"),
-                    columns[vector_blocks[v][0]][:, 2 * half + g : 2 * half + g + 1, :].to_broadcast([P, P, 4]),
-                    MULT,
+        def turn_picked(b, g):
+            turned[b, g] = turn_bank()
+            for t in range(4):
+                nc.tensor.transpose(turned[b, g][:, t, :], picked[b, g][:, t:PASS:4], ident[:])
+
+        def multiply_out(b, g):
+            nc.vector.tensor_tensor(
+                grouped(b)[:, g, :].rearrange("p (c t) -> p c t", t=4),
+                turned[b, g][:].rearrange("p t c -> p c t"),
+                columns[blocks[b][0]][:, g : g + 1, :].to_broadcast([P, P, 4]),
+                MULT,
+            )
+
+        def quantise_dy(q, passes):
+            cols = slice(passes[0] * N_TILE, (passes[-1] + 1) * N_TILE)
+            nc.vector.quantize_mx(
+                out=dy_codes[q][:, cols].bitcast(E5M2),
+                scales=dy_scales[q][:, cols],
+                in_=dy_grouped[q][:, 4 * cols.start : 4 * cols.stop],
+            )
+
+        def quantise_x(j, passes):
+            cols = slice(passes[0] * P, (passes[-1] + 1) * P)
+            nc.vector.quantize_mx(
+                out=x_codes[j][:, cols].bitcast(E4M3),
+                scales=x_scales[j][:, cols],
+                in_=x_grouped[j][:, passes[0] * PASS : (passes[-1] + 1) * PASS],
+            )
+            return x_grouped[j]
+
+        sum_count = []
+
+        def sum_bank():
+            sum_count.append(0)
+            return banks[PASSES + len(sum_count) % SUM_BANKS][:].rearrange("p a c -> p (a c)")
+
+        def product(bank, pairs, passes, opens, closes):
+            order = [(i, j, q, g) for i, (j, q) in enumerate(pairs) for g in passes]
+            for i, j, q, g in order:
+                nc.tensor.matmul_mx(
+                    out=bank[:, i * N_TILE : (i + 1) * N_TILE],
+                    lhsT=x_codes[j][:, g * P : (g + 1) * P].bitcast(E4M3),
+                    lhsT_scale=x_scales[j][:, g * P : (g + 1) * P],
+                    rhs=dy_codes[q][:, g * N_TILE : (g + 1) * N_TILE].bitcast(E5M2),
+                    rhs_scale=dy_scales[q][:, g * N_TILE : (g + 1) * N_TILE],
+                    start=(opens and (i, j, q, g) == order[0]),
+                    stop=(closes and (i, j, q, g) == order[-1]),
                 )
 
-        waiting = []
-
-        def quantise(name, block, grouped):
-            if name == "x":
-                x_codes[block] = keep.tile([P, PASSES * P], U32, name="x_codes%d" % block, align_bytes=64)
-                x_scales[block] = keep.tile([P, PASSES * P], U8, name="x_scales%d" % block, align_bytes=64)
-                nc.vector.quantize_mx(out=x_codes[block][:].bitcast(E4M3), scales=x_scales[block][:], in_=grouped[:])
+        def store(bank, pairs, copy):
+            width = len(pairs) * N_TILE
+            result = ring.tile([P, 2 * N_TILE], F32, name="result", bufs=4)
+            copy(result[:, :width], bank[:, :width])
+            j, q = pairs[0]
+            if pairs[-1][0] == j:
+                nc.sync.dma_start(out[j * P : (j + 1) * P, q * N_TILE : q * N_TILE + width], result[:, :width])
             else:
-                codes = ring.tile([P, PASSES * P], U32, name="dy_codes", align_bytes=64)
-                scales = ring.tile([P, PASSES * P], U8, name="dy_scales", align_bytes=64)
-                nc.vector.quantize_mx(out=codes[:].bitcast(E5M2), scales=scales[:], in_=grouped[:])
-                waiting.append((block, codes, scales))
-            if len(x_codes) == X_BLOCKS:
-                for job in waiting:
-                    product(*job)
-                waiting.clear()
+                rows_out = out[j * P : (j + 2) * P, q * N_TILE : (q + 1) * N_TILE]
+                nc.sync.dma_start(rows_out.rearrange("(i p) c -> p i c", i=2), result[:].rearrange("p (i c) -> p i c", i=2))
 
-        def product(block, codes, scales):
-            acc = psum.tile([P, X_BLOCKS, P], F32, name="acc")
-            for j in range(X_BLOCKS):
-                for g in range(PASSES):
-                    cols = slice(g * P, (g + 1) * P)
-                    nc.tensor.matmul_mx(
-                        out=acc[:, j, :],
-                        lhsT=x_codes[j][:, cols].bitcast(E4M3),
-                        lhsT_scale=x_scales[j][:, cols],
-                        rhs=codes[:, cols].bitcast(E5M2),
-                        rhs_scale=scales[:, cols],
-                        start=(g == 0),
-                        stop=(g == PASSES - 1),
-                    )
-            pending.append((block, acc))
+        x_ready, dy_ready, made = [], [], set()
 
-        def store_pending():
-            for block, acc in pending:
-                result = ring.tile([P, X_BLOCKS, P], F32, name="result")
-                nc.scalar.copy(result[:], acc[:])
-                nc.sync.dma_start(out[:, block * P : (block + 1) * P].rearrange("(j p) c -> p j c", p=P), result[:])
-            pending.clear()
+        def products_due():
+            todo = [(j, q) for j in x_ready for q in dy_ready if (j, q) not in made]
+            made.update(todo)
+            for a in range(0, len(todo), 2):
+                bank = sum_bank()
+                product(bank, todo[a : a + 2], every, True, True)
+                store(bank, todo[a : a + 2], nc.scalar.copy)
 
-        rounds = len(scalar_blocks)
-        for r in range(rounds + 2):
-            if r < rounds:
-                scalar_gather(2 * r)
-                vector_gather_and_turn(r)
-            if 1 <= r <= rounds:
-                multiply_and_turn(2 * r - 1)
-                weave(2 * r - 2)
-            if r < rounds:
-                scalar_gather(2 * r + 1)
-                multiply_out(r)
-            if 1 <= r <= rounds:
-                weave(2 * r - 1)
-            if r < rounds and r % 2 == 1:
-                quantise(*vector_blocks[r // 2], v_grouped[r // 2])
-            if r < rounds:
-                multiply_and_turn(2 * r)
-            store_pending()
-            if 1 <= r <= rounds:
-                quantise(*scalar_blocks[r - 1], s_grouped[r - 1])
+        every = range(PASSES)
+        def quantise(b):
+            name, block = blocks[b]
+            if name == "x":
+                quantise_x(block, every)
+                x_ready.append(block)
+                rooms.extend(x_grouped[block][:, i * PASS : (i + 1) * PASS] for i in range(X_BATCH))
+            elif block % 2 == 1:
+                quantise_dy(block // 2, every)
+                dy_ready.append(block // 2)
+                rooms.extend(dy_grouped[block // 2][:, i * PASS : (i + 1) * PASS] for i in range(DY_BATCH))
+
+        q = QUARTERS - 1
+        scalar_lane()
+        waiting = None
+        for b in range(len(blocks)):
+            road = ROADS[b]
+            vector_gather_and_turn(b, 2 if road[2] == "C" else 3)
+            if waiting:
+                multiply_out(*waiting)
+                quantise(b - 1)
+                scalar_lane()
+            if road[2] == "B":
+                turn_picked(b, 2)
+                turn_and_weave(b, 0, 2)
+                multiply_out(b, 3)
+                waiting = (b, 2)
+            else:
+                if b >= LATE:
+                    turn_and_weave(b, 0, 2)
+                if b == last:
+                    quantise_dy(q, range(2))
+                vector_gather_and_turn(b, 3)
+                if b < LATE:
+                    turn_and_weave(b, 0, 2)
+                multiply_out(b, 2)
+                waiting = (b, 3)
+            if b < last and ROADS[b + 1][2] == "B":
+                gather_third(b + 1)
+            products_due()
+        halves = [(sum_bank(), [(2 * h, q), (2 * h + 1, q)]) for h in range(2)]
+        for bank, pairs in halves:
+            product(bank, pairs, range(2), True, False)
+        quantise_dy(q, range(2, 3))
+        for bank, pairs in halves:
+            product(bank, pairs, range(2, 3), False, False)
+        multiply_out(last, 3)
+        quantise_dy(q, range(3, PASSES))
+        for bank, pairs in halves:
+            product(bank, pairs, range(3, PASSES), False, True)
+        store(*halves[0], nc.vector.tensor_copy)
+        store(*halves[1], nc.scalar.copy)

@@ -31,8 +31,9 @@ PICKED = 3
 THREE = (3, 6, 9)
 DEALT = 3
 LATE = 3
+AHEAD = 10
 FIRST_BATCH = 4
-DY_BATCH = 2
+DY_BATCH = 3
 X_BATCH = 4
 ROADS = ["FFBC" if b in THREE else "FFCC" for b in range(12)]
 ORDER = ["x", "dy", "dy"] * 4
@@ -112,7 +113,7 @@ def tile_attend_gmw_kernel(tc, xT, dyT, sw, tw, offs, offs2, out):
             return lists[blocks[b][0]][:, g * PASS // 16 : (g + 1) * PASS // 16]
 
         picked, rounded, turned = {}, {}, {}
-        dealt_count, slot_count, turn_count, room_count = [], [], [], []
+        dealt_count, slot_count, turn_count, woven = [], [], [], []
         rooms = [keep.tile([P, PASS], BF16, name="room%d" % i)[:] for i in range(FIRST_BATCH)]
         units = [(b, g) for b in range(len(blocks)) for g in range(2)]
 
@@ -138,15 +139,21 @@ def tile_attend_gmw_kernel(tc, xT, dyT, sw, tw, offs, offs2, out):
             nc.scalar.activation(picked[b, 2][:], windows[b][:].indirect(offsets(b, 2)), COPY)
 
         def turn_and_weave(b, g, count):
-            bank = turn_bank()
+            if b in woven:
+                return
+            woven.append(b)
+            bank = turn_bank()[:].rearrange("p a c -> p (a c)").rearrange("p (g c u) -> p g c u", g=2, u=2)
             for i in range(count):
                 words = rounded[b, g + i].bitcast(F32)
                 for u in range(2):
-                    nc.tensor.transpose(bank[:, 2 * i + u, :], words[:, u : 2 * P : 2], ident[:])
+                    nc.tensor.transpose(bank[:, i, :, u], words[:, u : 2 * P : 2], ident[:])
             nc.scalar.copy(
-                grouped(b)[:, g : g + count, :].bitcast(F32).rearrange("p g (c i u) -> p g c u i", i=2, u=2),
-                bank[:, : 2 * count, :].rearrange("p (g u) (c i) -> p g c u i", u=2, i=2),
+                grouped(b)[:, g : g + count, :].bitcast(F32),
+                bank[:, :count].rearrange("p g c u -> p g (c u)"),
             )
+
+        def woven_view(bank):
+            return bank[:].rearrange("p a c -> p (a c)").rearrange("p (c t) -> p c t", t=4)
 
         def vector_gather_and_turn(b, g):
             dealt = v_slots[len(dealt_count) % DEALT]
@@ -158,17 +165,17 @@ def tile_attend_gmw_kernel(tc, xT, dyT, sw, tw, offs, offs2, out):
             turned[b, g] = turn_bank()
             for u in range(2):
                 for w in range(2):
-                    nc.tensor.transpose(turned[b, g][:, 2 * u + w, :], dealt[:, 2 * P * u + w : 2 * P * (u + 1) : 2], ident[:])
+                    nc.tensor.transpose(woven_view(turned[b, g])[:, :, 2 * u + w], dealt[:, 2 * P * u + w : 2 * P * (u + 1) : 2], ident[:])
 
         def turn_picked(b, g):
             turned[b, g] = turn_bank()
             for t in range(4):
-                nc.tensor.transpose(turned[b, g][:, t, :], picked[b, g][:, t:PASS:4], ident[:])
+                nc.tensor.transpose(woven_view(turned[b, g])[:, :, t], picked[b, g][:, t:PASS:4], ident[:])
 
         def multiply_out(b, g):
             nc.vector.tensor_tensor(
                 grouped(b)[:, g, :].rearrange("p (c t) -> p c t", t=4),
-                turned[b, g][:].rearrange("p t c -> p c t"),
+                woven_view(turned[b, g]),
                 columns[blocks[b][0]][:, g : g + 1, :].to_broadcast([P, P, 4]),
                 MULT,
             )
@@ -236,7 +243,8 @@ def tile_attend_gmw_kernel(tc, xT, dyT, sw, tw, offs, offs2, out):
             if name == "x":
                 quantise_x(block, every)
                 x_ready.append(block)
-                rooms.extend(x_grouped[block][:, i * PASS : (i + 1) * PASS] for i in range(X_BATCH))
+                rooms.extend(x_grouped[block][:, i * PASS : (i + 1) * PASS] for i in range(min(X_BATCH, PASSES)))
+                rooms.extend(keep.tile([P, PASS], BF16, name="room_x%d_%d" % (block, i))[:] for i in range(PASSES, X_BATCH))
             elif block % 2 == 1:
                 quantise_dy(block // 2, every)
                 dy_ready.append(block // 2)
@@ -255,6 +263,8 @@ def tile_attend_gmw_kernel(tc, xT, dyT, sw, tw, offs, offs2, out):
             if road[2] == "B":
                 turn_picked(b, 2)
                 turn_and_weave(b, 0, 2)
+                if b == last:
+                    quantise_dy(q, range(2))
                 multiply_out(b, 3)
                 waiting = (b, 2)
             else:
@@ -267,18 +277,21 @@ def tile_attend_gmw_kernel(tc, xT, dyT, sw, tw, offs, offs2, out):
                     turn_and_weave(b, 0, 2)
                 multiply_out(b, 2)
                 waiting = (b, 3)
+            if AHEAD <= b < last:
+                turn_and_weave(b + 1, 0, 2)
             if b < last and ROADS[b + 1][2] == "B":
                 gather_third(b + 1)
             products_due()
         halves = [(sum_bank(), [(2 * h, q), (2 * h + 1, q)]) for h in range(2)]
         for bank, pairs in halves:
             product(bank, pairs, range(2), True, False)
-        quantise_dy(q, range(2, 3))
+        final = waiting[1]
+        quantise_dy(q, [5 - final])
         for bank, pairs in halves:
-            product(bank, pairs, range(2, 3), False, False)
-        multiply_out(last, 3)
-        quantise_dy(q, range(3, PASSES))
+            product(bank, pairs, [5 - final], False, False)
+        multiply_out(last, final)
+        quantise_dy(q, [final])
         for bank, pairs in halves:
-            product(bank, pairs, range(3, PASSES), False, True)
+            product(bank, pairs, [final], False, True)
         store(*halves[0], nc.vector.tensor_copy)
         store(*halves[1], nc.scalar.copy)

@@ -23,20 +23,17 @@ PASSES = E // PASS
 WINDOW = 704
 X_BLOCKS = D // P
 DY_BLOCKS = DV // P
-N_TILE = 256
-QUARTERS = DV // N_TILE
 SUM_BANKS = 4
 TURN_BANKS = 4
 PICKED = 3
 THREE = (3, 6, 9)
 DEALT = 3
 LATE = 3
-AHEAD = 10
+AHEAD = 11
 FIRST_BATCH = 4
-DY_BATCH = 3
-X_BATCH = 4
+BATCH = 2
 ROADS = ["FFBC" if b in THREE else "FFCC" for b in range(12)]
-ORDER = ["x", "dy", "dy"] * 4
+ORDER = ["x", "dy"] * 4 + ["dy"] * 4
 WARM = 1
 
 
@@ -59,7 +56,7 @@ def tile_attend_gmw_kernel(tc, xT, dyT, sw, tw, offs, offs2, out):
             for g in range(PASSES)
             if any(ROADS[b][g] in "EF" and ORDER[b] == name for b in range(len(ORDER)))
         }
-        columns = {name: keep.tile([P, PASSES, 4], F32, name="columns_" + name) for name in ("x", "dy")}
+        columns = {name: keep.tile([P, 2, 4], F32, name="columns_" + name) for name in ("x", "dy")}
         windows = [keep.tile([P, WINDOW], F32, name="window%d" % b) for b in range(len(blocks))]
         ident = keep.tile([P, P], F32, name="ident")
         banks = [psum.tile([P, 4, P], F32, name="bank%d" % i) for i in range(PASSES + SUM_BANKS)]
@@ -69,7 +66,7 @@ def tile_attend_gmw_kernel(tc, xT, dyT, sw, tw, offs, offs2, out):
             nc.sync.dma_start(windows[b][:, :V], table[name][block * P : (block + 1) * P, :])
 
         def load_columns(name):
-            nc.sync.dma_start(columns[name][:], weights[name][0:1, :].rearrange("o (g p t) -> p (o g) t", p=P, t=4))
+            nc.sync.dma_start(columns[name][:], weights[name][0:1, 2 * PASS :].rearrange("o (g p t) -> p (o g) t", p=P, t=4))
 
         def load_rows(name, g):
             nc.sync.dma_start(rows[name, g][:], weights[name][:, g * PASS : (g + 1) * PASS])
@@ -94,20 +91,14 @@ def tile_attend_gmw_kernel(tc, xT, dyT, sw, tw, offs, offs2, out):
             warm = keep.tile([P, 1], F32, name="warm")
             nc.scalar.activation(warm[:], windows[0][:, V : V + 1], COPY)
 
-        dy_grouped = [keep.tile([P, 2 * PASSES * PASS], BF16, name="dy_grouped%d" % q, align_bytes=64) for q in range(QUARTERS)]
-        dy_codes = [keep.tile([P, PASSES * N_TILE], U32, name="dy_codes%d" % q, align_bytes=64) for q in range(QUARTERS)]
-        dy_scales = [keep.tile([P, PASSES * N_TILE], U8, name="dy_scales%d" % q, align_bytes=64) for q in range(QUARTERS)]
-        x_grouped = [keep.tile([P, PASSES * PASS], BF16, name="x_grouped%d" % j, align_bytes=64) for j in range(X_BLOCKS)]
-        x_codes = [keep.tile([P, PASSES * P], U32, name="x_codes%d" % j, align_bytes=64) for j in range(X_BLOCKS)]
-        x_scales = [keep.tile([P, PASSES * P], U8, name="x_scales%d" % j, align_bytes=64) for j in range(X_BLOCKS)]
+        laid = [keep.tile([P, E], BF16, name="laid%d" % b, align_bytes=64) for b in range(len(blocks))]
+        codes = {key: keep.tile([P, PASSES * P], U32, name="codes_%s%d" % key, align_bytes=64) for key in blocks}
+        scales = {key: keep.tile([P, PASSES * P], U8, name="scales_%s%d" % key, align_bytes=64) for key in blocks}
         s_slots = [keep.tile([P, PASS], F32, name="s_slot%d" % i) for i in range(PICKED)]
         v_slots = [keep.tile([P, PASS], F32, name="v_slot%d" % i) for i in range(DEALT)]
 
         def grouped(b):
-            name, block = blocks[b]
-            if name == "x":
-                return x_grouped[block][:].rearrange("p (g c) -> p g c", g=PASSES)
-            return dy_grouped[block // 2][:].rearrange("p (g m c) -> p g m c", g=PASSES, m=2)[:, :, block % 2, :]
+            return laid[b][:].rearrange("p (g c) -> p g c", g=PASSES)
 
         def offsets(b, g):
             return lists[blocks[b][0]][:, g * PASS // 16 : (g + 1) * PASS // 16]
@@ -176,81 +167,59 @@ def tile_attend_gmw_kernel(tc, xT, dyT, sw, tw, offs, offs2, out):
             nc.vector.tensor_tensor(
                 grouped(b)[:, g, :].rearrange("p (c t) -> p c t", t=4),
                 woven_view(turned[b, g]),
-                columns[blocks[b][0]][:, g : g + 1, :].to_broadcast([P, P, 4]),
+                columns[blocks[b][0]][:, g - 2 : g - 1, :].to_broadcast([P, P, 4]),
                 MULT,
             )
 
-        def quantise_dy(q, passes):
-            cols = slice(passes[0] * N_TILE, (passes[-1] + 1) * N_TILE)
-            nc.vector.quantize_mx(
-                out=dy_codes[q][:, cols].bitcast(E5M2),
-                scales=dy_scales[q][:, cols],
-                in_=dy_grouped[q][:, 4 * cols.start : 4 * cols.stop],
-            )
-
-        def quantise_x(j, passes):
+        def quantise(b, passes):
             cols = slice(passes[0] * P, (passes[-1] + 1) * P)
             nc.vector.quantize_mx(
-                out=x_codes[j][:, cols].bitcast(E4M3),
-                scales=x_scales[j][:, cols],
-                in_=x_grouped[j][:, passes[0] * PASS : (passes[-1] + 1) * PASS],
+                out=codes[blocks[b]][:, cols].bitcast(E4M3 if blocks[b][0] == "x" else E5M2),
+                scales=scales[blocks[b]][:, cols],
+                in_=laid[b][:, 4 * cols.start : 4 * cols.stop],
             )
-            return x_grouped[j]
 
         sum_count = []
 
         def sum_bank():
             sum_count.append(0)
-            return banks[PASSES + len(sum_count) % SUM_BANKS][:].rearrange("p a c -> p (a c)")
+            return banks[TURN_BANKS + len(sum_count) % SUM_BANKS]
 
         def product(bank, pairs, passes, opens, closes):
-            order = [(i, j, q, g) for i, (j, q) in enumerate(pairs) for g in passes]
-            for i, j, q, g in order:
+            order = [(i, j, m, g) for i, (j, m) in enumerate(pairs) for g in passes]
+            for i, j, m, g in order:
+                cols = slice(g * P, (g + 1) * P)
                 nc.tensor.matmul_mx(
-                    out=bank[:, i * N_TILE : (i + 1) * N_TILE],
-                    lhsT=x_codes[j][:, g * P : (g + 1) * P].bitcast(E4M3),
-                    lhsT_scale=x_scales[j][:, g * P : (g + 1) * P],
-                    rhs=dy_codes[q][:, g * N_TILE : (g + 1) * N_TILE].bitcast(E5M2),
-                    rhs_scale=dy_scales[q][:, g * N_TILE : (g + 1) * N_TILE],
-                    start=(opens and (i, j, q, g) == order[0]),
-                    stop=(closes and (i, j, q, g) == order[-1]),
+                    out=bank[:, i, :],
+                    lhsT=codes["x", j][:, cols].bitcast(E4M3),
+                    lhsT_scale=scales["x", j][:, cols],
+                    rhs=codes["dy", m][:, cols].bitcast(E5M2),
+                    rhs_scale=scales["dy", m][:, cols],
+                    start=(opens and (i, j, m, g) == order[0]),
+                    stop=(closes and (i, j, m, g) == order[-1]),
                 )
 
-        def store(bank, pairs, copy):
-            width = len(pairs) * N_TILE
-            result = ring.tile([P, 2 * N_TILE], F32, name="result", bufs=4)
-            copy(result[:, :width], bank[:, :width])
-            j, q = pairs[0]
-            if pairs[-1][0] == j:
-                nc.sync.dma_start(out[j * P : (j + 1) * P, q * N_TILE : q * N_TILE + width], result[:, :width])
+        def store(bank, pairs, copy, queue):
+            count = len(pairs)
+            result = ring.tile([P, 4, P], F32, name="result", bufs=4)
+            copy(result[:, :count, :], bank[:, :count, :])
+            (j, m), (j_end, m_end) = pairs[0], pairs[-1]
+            target = out[j * P : (j_end + 1) * P, m * P : (m_end + 1) * P]
+            if j_end == j:
+                queue.dma_start(target.rearrange("p (i c) -> p i c", c=P), result[:, :count, :])
             else:
-                rows_out = out[j * P : (j + 2) * P, q * N_TILE : (q + 1) * N_TILE]
-                nc.sync.dma_start(rows_out.rearrange("(i p) c -> p i c", i=2), result[:].rearrange("p (i c) -> p i c", i=2))
+                queue.dma_start(target.rearrange("(i p) c -> p i c", p=P), result[:, :count, :])
 
-        x_ready, dy_ready, made = [], [], set()
-
-        def products_due():
-            todo = [(j, q) for j in x_ready for q in dy_ready if (j, q) not in made]
-            made.update(todo)
-            for a in range(0, len(todo), 2):
+        def products(b):
+            name, index = blocks[b]
+            others = [other for kind, other in blocks[:b] if kind != name]
+            pairs = [(index, other) if name == "x" else (other, index) for other in others]
+            if pairs:
                 bank = sum_bank()
-                product(bank, todo[a : a + 2], every, True, True)
-                store(bank, todo[a : a + 2], nc.scalar.copy)
+                product(bank, pairs, every, True, True)
+                store(bank, pairs, nc.scalar.copy, nc.sync)
 
         every = range(PASSES)
-        def quantise(b):
-            name, block = blocks[b]
-            if name == "x":
-                quantise_x(block, every)
-                x_ready.append(block)
-                rooms.extend(x_grouped[block][:, i * PASS : (i + 1) * PASS] for i in range(min(X_BATCH, PASSES)))
-                rooms.extend(keep.tile([P, PASS], BF16, name="room_x%d_%d" % (block, i))[:] for i in range(PASSES, X_BATCH))
-            elif block % 2 == 1:
-                quantise_dy(block // 2, every)
-                dy_ready.append(block // 2)
-                rooms.extend(dy_grouped[block // 2][:, i * PASS : (i + 1) * PASS] for i in range(DY_BATCH))
-
-        q = QUARTERS - 1
         scalar_lane()
         waiting = None
         for b in range(len(blocks)):
@@ -258,20 +227,17 @@ def tile_attend_gmw_kernel(tc, xT, dyT, sw, tw, offs, offs2, out):
             vector_gather_and_turn(b, 2 if road[2] == "C" else 3)
             if waiting:
                 multiply_out(*waiting)
-                quantise(b - 1)
+                quantise(b - 1, every)
+                rooms.extend(laid[b - 1][:, i * PASS : (i + 1) * PASS] for i in range(BATCH))
                 scalar_lane()
             if road[2] == "B":
                 turn_picked(b, 2)
                 turn_and_weave(b, 0, 2)
-                if b == last:
-                    quantise_dy(q, range(2))
                 multiply_out(b, 3)
                 waiting = (b, 2)
             else:
                 if b >= LATE:
                     turn_and_weave(b, 0, 2)
-                if b == last:
-                    quantise_dy(q, range(2))
                 vector_gather_and_turn(b, 3)
                 if b < LATE:
                     turn_and_weave(b, 0, 2)
@@ -281,17 +247,17 @@ def tile_attend_gmw_kernel(tc, xT, dyT, sw, tw, offs, offs2, out):
                 turn_and_weave(b + 1, 0, 2)
             if b < last and ROADS[b + 1][2] == "B":
                 gather_third(b + 1)
-            products_due()
-        halves = [(sum_bank(), [(2 * h, q), (2 * h + 1, q)]) for h in range(2)]
+            if b >= 1:
+                products(b - 1)
+        m = DY_BLOCKS - 1
+        halves = [(sum_bank(), [(2 * h, m), (2 * h + 1, m)]) for h in range(2)]
+        quantise(last, range(2))
+        quantise(last, range(2, 3))
         for bank, pairs in halves:
-            product(bank, pairs, range(2), True, False)
-        final = waiting[1]
-        quantise_dy(q, [5 - final])
+            product(bank, pairs, range(3), True, False)
+        multiply_out(last, 3)
+        quantise(last, range(3, PASSES))
         for bank, pairs in halves:
-            product(bank, pairs, [5 - final], False, False)
-        multiply_out(last, final)
-        quantise_dy(q, [final])
-        for bank, pairs in halves:
-            product(bank, pairs, [final], False, True)
-        store(*halves[0], nc.vector.tensor_copy)
-        store(*halves[1], nc.scalar.copy)
+            product(bank, pairs, range(3, PASSES), False, True)
+        store(*halves[0], nc.vector.tensor_copy, nc.sync)
+        store(*halves[1], nc.scalar.copy, nc.scalar)

@@ -133,18 +133,18 @@ def tile_attend_gmw_kernel(tc, xT, dyT, sw, tw, offs, offs2, out):
             if b in woven:
                 return
             woven.append(b)
-            bank = turn_bank()[:].rearrange("p a c -> p (a c)").rearrange("p (g c u) -> p g c u", g=2, u=2)
+            bank = turn_bank()[:].rearrange("p a c -> p (a c)").rearrange("p (g c u i) -> p g c u i", g=2, u=2, i=2)
             for i in range(count):
                 words = rounded[b, g + i].bitcast(F32)
                 for u in range(2):
-                    nc.tensor.transpose(bank[:, i, :, u], words[:, u : 2 * P : 2], ident[:])
+                    nc.tensor.transpose(bank[:, i, :, u, :], words[:, u : 2 * P : 2], ident[:])
             nc.scalar.copy(
-                grouped(b)[:, g : g + count, :].bitcast(F32),
-                bank[:, :count].rearrange("p g c u -> p g (c u)"),
+                grouped(b)[:, g : g + count, :].bitcast(F32).rearrange("p g (c i u) -> p (g c) u i", i=2, u=2),
+                bank[:, :count].rearrange("p g c u i -> p (g c) u i"),
             )
 
         def woven_view(bank):
-            return bank[:].rearrange("p a c -> p (a c)").rearrange("p (c t) -> p c t", t=4)
+            return bank[:].rearrange("p a c -> p (a c)").rearrange("p (c t i) -> p c t i", t=4, i=2)
 
         def vector_gather_and_turn(b, g):
             dealt = v_slots[len(dealt_count) % DEALT]
@@ -156,18 +156,18 @@ def tile_attend_gmw_kernel(tc, xT, dyT, sw, tw, offs, offs2, out):
             turned[b, g] = turn_bank()
             for u in range(2):
                 for w in range(2):
-                    nc.tensor.transpose(woven_view(turned[b, g])[:, :, 2 * u + w], dealt[:, 2 * P * u + w : 2 * P * (u + 1) : 2], ident[:])
+                    nc.tensor.transpose(woven_view(turned[b, g])[:, :, 2 * u + w, :], dealt[:, 2 * P * u + w : 2 * P * (u + 1) : 2], ident[:])
 
         def turn_picked(b, g):
             turned[b, g] = turn_bank()
             for t in range(4):
-                nc.tensor.transpose(woven_view(turned[b, g])[:, :, t], picked[b, g][:, t:PASS:4], ident[:])
+                nc.tensor.transpose(woven_view(turned[b, g])[:, :, t, :], picked[b, g][:, t:PASS:4], ident[:])
 
         def multiply_out(b, g):
             nc.vector.tensor_tensor(
-                grouped(b)[:, g, :].rearrange("p (c t) -> p c t", t=4),
+                grouped(b)[:, g, :].rearrange("p (c i t) -> p c t i", i=2, t=4),
                 woven_view(turned[b, g]),
-                columns[blocks[b][0]][:, g - 2 : g - 1, :].to_broadcast([P, P, 4]),
+                columns[blocks[b][0]][:, g - 2 : g - 1, :].unsqueeze(3).to_broadcast([P, P // 2, 4, 2]),
                 MULT,
             )
 

@@ -25,13 +25,13 @@ X_BLOCKS = D // P
 DY_BLOCKS = DV // P
 SUM_BANKS = 4
 TURN_BANKS = 4
-PICKED = 3
+PICKED = 2
 THREE = (3, 6, 9)
 DEALT = 3
 LATE = 3
 AHEAD = 11
-FIRST_BATCH = 4
-BATCH = 2
+FIRST_BATCH = 2
+SPLIT = 1
 ROADS = ["FFBC" if b in THREE else "FFCC" for b in range(12)]
 ORDER = ["x", "dy"] * 4 + ["dy"] * 4
 WARM = 1
@@ -50,12 +50,7 @@ def tile_attend_gmw_kernel(tc, xT, dyT, sw, tw, offs, offs2, out):
         psum = ctx.enter_context(tc.psum_pool(name="psum", bufs=1))
 
         lists = {name: keep.tile([P, E // 16], U16, name="list_" + name) for name in ("x", "dy")}
-        rows = {
-            (name, g): keep.tile([P, PASS], F32, name="rows_%s%d" % (name, g))
-            for name in ("dy", "x")
-            for g in range(PASSES)
-            if any(ROADS[b][g] in "EF" and ORDER[b] == name for b in range(len(ORDER)))
-        }
+        rows = {name: keep.tile([P, 2 * PASS], F32, name="rows_" + name) for name in ("x", "dy")}
         columns = {name: keep.tile([P, 2, 4], F32, name="columns_" + name) for name in ("x", "dy")}
         windows = [keep.tile([P, WINDOW], F32, name="window%d" % b) for b in range(len(blocks))]
         ident = keep.tile([P, P], F32, name="ident")
@@ -69,7 +64,7 @@ def tile_attend_gmw_kernel(tc, xT, dyT, sw, tw, offs, offs2, out):
             nc.sync.dma_start(columns[name][:], weights[name][0:1, 2 * PASS :].rearrange("o (g p t) -> p (o g) t", p=P, t=4))
 
         def load_rows(name, g):
-            nc.sync.dma_start(rows[name, g][:], weights[name][:, g * PASS : (g + 1) * PASS])
+            nc.sync.dma_start(rows[name][:, g * PASS : (g + 1) * PASS], weights[name][:, g * PASS : (g + 1) * PASS])
 
         nc.sync.dma_start(lists["x"][:], offs)
         load_block(0)
@@ -94,7 +89,7 @@ def tile_attend_gmw_kernel(tc, xT, dyT, sw, tw, offs, offs2, out):
         laid = [keep.tile([P, E], BF16, name="laid%d" % b, align_bytes=64) for b in range(len(blocks))]
         codes = {key: keep.tile([P, PASSES * P], U32, name="codes_%s%d" % key, align_bytes=64) for key in blocks}
         scales = {key: keep.tile([P, PASSES * P], U8, name="scales_%s%d" % key, align_bytes=64) for key in blocks}
-        s_slots = [keep.tile([P, PASS], F32, name="s_slot%d" % i) for i in range(PICKED)]
+        s_slots = [keep.tile([P, 2 * PASS], F32, name="s_slot%d" % i) for i in range(PICKED)]
         v_slots = [keep.tile([P, PASS], F32, name="v_slot%d" % i) for i in range(DEALT)]
 
         def grouped(b):
@@ -105,24 +100,26 @@ def tile_attend_gmw_kernel(tc, xT, dyT, sw, tw, offs, offs2, out):
 
         picked, rounded, turned = {}, {}, {}
         dealt_count, slot_count, turn_count, woven = [], [], [], []
-        rooms = [keep.tile([P, PASS], BF16, name="room%d" % i)[:] for i in range(FIRST_BATCH)]
-        units = [(b, g) for b in range(len(blocks)) for g in range(2)]
+        rooms = [keep.tile([P, 2 * PASS], BF16, name="room%d" % i)[:] for i in range(FIRST_BATCH)]
+        units = list(range(len(blocks)))
 
         def turn_bank():
             turn_count.append(0)
             return banks[len(turn_count) % TURN_BANKS]
 
-        def scalar_gather(b, g):
-            picked[b, g] = s_slots[len(slot_count) % PICKED]
-            slot_count.append(0)
-            nc.scalar.activation(picked[b, g][:], windows[b][:].indirect(offsets(b, g)), COPY)
-
         def scalar_lane():
             while rooms and units:
-                b, g = units.pop(0)
-                scalar_gather(b, g)
-                rounded[b, g] = rooms.pop(0)
-                nc.gpsimd.tensor_tensor(rounded[b, g], picked[b, g][:], rows[blocks[b][0], g][:], MULT)
+                b = units.pop(0)
+                pair = s_slots[b % PICKED]
+                room = rooms.pop(0)
+                for g in range(2):
+                    cols = slice(g * PASS, (g + 1) * PASS)
+                    nc.scalar.activation(pair[:, cols], windows[b][:].indirect(offsets(b, g)), COPY)
+                    rounded[b, g] = room[:, cols]
+                    if b < SPLIT:
+                        nc.gpsimd.tensor_tensor(room[:, cols], pair[:, cols], rows[blocks[b][0]][:, cols], MULT)
+                if b >= SPLIT:
+                    nc.gpsimd.tensor_tensor(room, pair[:], rows[blocks[b][0]][:], MULT)
 
         def gather_third(b):
             picked[b, 2] = v_slots[len(dealt_count) % DEALT]
@@ -219,6 +216,11 @@ def tile_attend_gmw_kernel(tc, xT, dyT, sw, tw, offs, offs2, out):
                 product(bank, pairs, every, True, True)
                 store(bank, pairs, nc.scalar.copy, nc.sync)
 
+        def quantise_and_release(b):
+            quantise(b, every)
+            rooms.append(laid[b][:, : 2 * PASS])
+            scalar_lane()
+
         every = range(PASSES)
         scalar_lane()
         waiting = None
@@ -227,9 +229,7 @@ def tile_attend_gmw_kernel(tc, xT, dyT, sw, tw, offs, offs2, out):
             vector_gather_and_turn(b, 2 if road[2] == "C" else 3)
             if waiting:
                 multiply_out(*waiting)
-                quantise(b - 1, every)
-                rooms.extend(laid[b - 1][:, i * PASS : (i + 1) * PASS] for i in range(BATCH))
-                scalar_lane()
+                quantise_and_release(b - 1)
             if road[2] == "B":
                 turn_picked(b, 2)
                 turn_and_weave(b, 0, 2)

@@ -23,18 +23,15 @@ PASSES = E // PASS
 WINDOW = 704
 X_BLOCKS = D // P
 DY_BLOCKS = DV // P
-SUM_BANKS = 4
-TURN_BANKS = 4
+BANKS = 8
 PICKED = 2
-THREE = (3, 6, 9)
 DEALT = 3
 LATE = 3
-AHEAD = 11
 FIRST_BATCH = 2
 SPLIT = 1
-ROADS = ["FFBC" if b in THREE else "FFCC" for b in range(12)]
+THREE = (3, 4, 6, 7, 9, 10)
+SHARE = 256
 ORDER = ["x", "dy"] * 4 + ["dy"] * 4
-WARM = 1
 
 
 def tile_attend_gmw_kernel(tc, xT, dyT, sw, tw, offs, offs2, out):
@@ -54,7 +51,7 @@ def tile_attend_gmw_kernel(tc, xT, dyT, sw, tw, offs, offs2, out):
         columns = {name: keep.tile([P, 2, 4], F32, name="columns_" + name) for name in ("x", "dy")}
         windows = [keep.tile([P, WINDOW], F32, name="window%d" % b) for b in range(len(blocks))]
         ident = keep.tile([P, P], F32, name="ident")
-        banks = [psum.tile([P, 4, P], F32, name="bank%d" % i) for i in range(PASSES + SUM_BANKS)]
+        free = [psum.tile([P, PASS], F32, name="bank%d" % i) for i in range(BANKS)]
 
         def load_block(b):
             name, block = blocks[b]
@@ -66,25 +63,20 @@ def tile_attend_gmw_kernel(tc, xT, dyT, sw, tw, offs, offs2, out):
         def load_rows(name, g):
             nc.sync.dma_start(rows[name][:, g * PASS : (g + 1) * PASS], weights[name][:, g * PASS : (g + 1) * PASS])
 
-        nc.sync.dma_start(lists["x"][:], offs)
-        load_block(0)
-        load_rows("x", 0)
-        load_columns("x")
-        load_rows("x", 1)
-        nc.sync.dma_start(lists["dy"][:], offs2)
-        load_block(1)
-        load_rows("dy", 0)
-        load_columns("dy")
-        load_rows("dy", 1)
+        for b, (name, index_list) in enumerate((("x", offs), ("dy", offs2))):
+            nc.sync.dma_start(lists[name][:], index_list)
+            load_block(b)
+            load_rows(name, 0)
+            load_columns(name)
+            load_rows(name, 1)
         for b in range(2, len(blocks)):
             load_block(b)
 
         for window in windows:
             nc.vector.memset(window[:, V:].bitcast(I32), 0)
         make_identity(nc, ident[:])
-        if WARM:
-            warm = keep.tile([P, 1], F32, name="warm")
-            nc.scalar.activation(warm[:], windows[0][:, V : V + 1], COPY)
+        warm = keep.tile([P, 1], F32, name="warm")
+        nc.scalar.activation(warm[:], windows[0][:, V : V + 1], COPY)
 
         laid = [keep.tile([P, E], BF16, name="laid%d" % b, align_bytes=64) for b in range(len(blocks))]
         codes = {key: keep.tile([P, PASSES * P], U32, name="codes_%s%d" % key, align_bytes=64) for key in blocks}
@@ -92,78 +84,85 @@ def tile_attend_gmw_kernel(tc, xT, dyT, sw, tw, offs, offs2, out):
         s_slots = [keep.tile([P, 2 * PASS], F32, name="s_slot%d" % i) for i in range(PICKED)]
         v_slots = [keep.tile([P, PASS], F32, name="v_slot%d" % i) for i in range(DEALT)]
 
-        def grouped(b):
-            return laid[b][:].rearrange("p (g c) -> p g c", g=PASSES)
-
         def offsets(b, g):
             return lists[blocks[b][0]][:, g * PASS // 16 : (g + 1) * PASS // 16]
 
-        picked, rounded, turned = {}, {}, {}
-        dealt_count, slot_count, turn_count, woven = [], [], [], []
+        picked, rounded, turned, home = {}, {}, {}, {}
+        emptied = []
         rooms = [keep.tile([P, 2 * PASS], BF16, name="room%d" % i)[:] for i in range(FIRST_BATCH)]
         units = list(range(len(blocks)))
 
-        def turn_bank():
-            turn_count.append(0)
-            return banks[len(turn_count) % TURN_BANKS]
+        def take(slots):
+            slots.append(slots.pop(0))
+            return slots[-1]
+
+        def scalar_gather(b, g, target):
+            nc.scalar.activation(target, windows[b][:].indirect(offsets(b, g)), COPY)
+
+        def gather_third(b):
+            picked[b, 2] = take(v_slots)
+            first = 2 * PASS // 16
+            nc.scalar.activation(
+                picked[b, 2][:, :SHARE], windows[b][:].indirect(lists[blocks[b][0]][:, first : first + SHARE // 16]), COPY
+            )
+
+        def gather_rest(b):
+            first = (2 * PASS + SHARE) // 16
+            nc.vector.tensor_copy(picked[b, 2][:, SHARE:], windows[b][:].indirect(lists[blocks[b][0]][:, first : 3 * PASS // 16]))
 
         def scalar_lane():
             while rooms and units:
                 b = units.pop(0)
-                pair = s_slots[b % PICKED]
+                pair = take(s_slots)
                 room = rooms.pop(0)
                 for g in range(2):
                     cols = slice(g * PASS, (g + 1) * PASS)
-                    nc.scalar.activation(pair[:, cols], windows[b][:].indirect(offsets(b, g)), COPY)
+                    scalar_gather(b, g, pair[:, cols])
                     rounded[b, g] = room[:, cols]
                     if b < SPLIT:
                         nc.gpsimd.tensor_tensor(room[:, cols], pair[:, cols], rows[blocks[b][0]][:, cols], MULT)
                 if b >= SPLIT:
                     nc.gpsimd.tensor_tensor(room, pair[:], rows[blocks[b][0]][:], MULT)
 
-        def gather_third(b):
-            picked[b, 2] = v_slots[len(dealt_count) % DEALT]
-            dealt_count.append(0)
-            nc.scalar.activation(picked[b, 2][:], windows[b][:].indirect(offsets(b, 2)), COPY)
-
         def turn_and_weave(b, g, count):
-            if b in woven:
-                return
-            woven.append(b)
-            bank = turn_bank()[:].rearrange("p a c -> p (a c)").rearrange("p (g c u i) -> p g c u i", g=2, u=2, i=2)
-            for i in range(count):
-                words = rounded[b, g + i].bitcast(F32)
+            whole = emptied.pop() if emptied else free[0]
+            free.remove(whole)
+            free.append(whole)
+            bank = whole[:].rearrange("p (c u i) -> p c u i", u=2, i=2)
+            for k in range(count):
+                words = rounded[b, g + k].bitcast(F32)
                 for u in range(2):
-                    nc.tensor.transpose(bank[:, i, :, u, :], words[:, u : 2 * P : 2], ident[:])
+                    nc.tensor.transpose(bank[:, k * P // 2 : (k + 1) * P // 2, u, :], words[:, u : 2 * P : 2], ident[:])
             nc.scalar.copy(
-                grouped(b)[:, g : g + count, :].bitcast(F32).rearrange("p g (c i u) -> p (g c) u i", i=2, u=2),
-                bank[:, :count].rearrange("p g c u i -> p (g c) u i"),
+                laid[b][:, g * PASS : (g + count) * PASS].bitcast(F32).rearrange("p (c i u) -> p c u i", i=2, u=2),
+                bank[:, : count * P // 2],
             )
 
-        def woven_view(bank):
-            return bank[:].rearrange("p a c -> p (a c)").rearrange("p (c t i) -> p c t i", t=4, i=2)
+        def turn_bank(b, g):
+            home[b, g] = take(free)
+            turned[b, g] = home[b, g][:].rearrange("p (c t i) -> p c t i", t=4, i=2)
+            return turned[b, g]
 
         def vector_gather_and_turn(b, g):
-            dealt = v_slots[len(dealt_count) % DEALT]
-            dealt_count.append(0)
+            dealt = take(v_slots)
             nc.vector.tensor_copy(
                 dealt[:].bitcast(U32).rearrange("f (u s w) -> f s u w", u=2, w=2),
                 windows[b][:].bitcast(U32).indirect(offsets(b, g)),
             )
-            turned[b, g] = turn_bank()
+            bank = turn_bank(b, g)
             for u in range(2):
                 for w in range(2):
-                    nc.tensor.transpose(woven_view(turned[b, g])[:, :, 2 * u + w, :], dealt[:, 2 * P * u + w : 2 * P * (u + 1) : 2], ident[:])
+                    nc.tensor.transpose(bank[:, :, 2 * u + w, :], dealt[:, 2 * P * u + w : 2 * P * (u + 1) : 2], ident[:])
 
         def turn_picked(b, g):
-            turned[b, g] = turn_bank()
+            bank = turn_bank(b, g)
             for t in range(4):
-                nc.tensor.transpose(woven_view(turned[b, g])[:, :, t, :], picked[b, g][:, t:PASS:4], ident[:])
+                nc.tensor.transpose(bank[:, :, t, :], picked[b, g][:, t:PASS:4], ident[:])
 
         def multiply_out(b, g):
             nc.vector.tensor_tensor(
-                grouped(b)[:, g, :].rearrange("p (c i t) -> p c t i", i=2, t=4),
-                woven_view(turned[b, g]),
+                laid[b][:, g * PASS : (g + 1) * PASS].rearrange("p (c i t) -> p c t i", i=2, t=4),
+                turned[b, g],
                 columns[blocks[b][0]][:, g - 2 : g - 1, :].unsqueeze(3).to_broadcast([P, P // 2, 4, 2]),
                 MULT,
             )
@@ -176,88 +175,79 @@ def tile_attend_gmw_kernel(tc, xT, dyT, sw, tw, offs, offs2, out):
                 in_=laid[b][:, 4 * cols.start : 4 * cols.stop],
             )
 
-        sum_count = []
+        def release(spent):
+            rooms.append(spent[:, : 2 * PASS])
+            scalar_lane()
 
-        def sum_bank():
-            sum_count.append(0)
-            return banks[TURN_BANKS + len(sum_count) % SUM_BANKS]
-
-        def product(bank, pairs, passes, opens, closes):
-            order = [(i, j, m, g) for i, (j, m) in enumerate(pairs) for g in passes]
-            for i, j, m, g in order:
+        def product(target, j, m, passes, opens, closes):
+            for g in passes:
                 cols = slice(g * P, (g + 1) * P)
                 nc.tensor.matmul_mx(
-                    out=bank[:, i, :],
+                    out=target,
                     lhsT=codes["x", j][:, cols].bitcast(E4M3),
                     lhsT_scale=scales["x", j][:, cols],
                     rhs=codes["dy", m][:, cols].bitcast(E5M2),
                     rhs_scale=scales["dy", m][:, cols],
-                    start=(opens and (i, j, m, g) == order[0]),
-                    stop=(closes and (i, j, m, g) == order[-1]),
+                    start=(opens and g == passes[0]),
+                    stop=(closes and g == passes[-1]),
                 )
 
         def store(bank, pairs, copy, queue):
-            count = len(pairs)
-            result = ring.tile([P, 4, P], F32, name="result", bufs=4)
-            copy(result[:, :count, :], bank[:, :count, :])
+            width = len(pairs) * P
+            result = ring.tile([P, PASS], F32, name="result", bufs=4)
+            copy(result[:, :width], bank[:, :width])
             (j, m), (j_end, m_end) = pairs[0], pairs[-1]
             target = out[j * P : (j_end + 1) * P, m * P : (m_end + 1) * P]
             if j_end == j:
-                queue.dma_start(target.rearrange("p (i c) -> p i c", c=P), result[:, :count, :])
+                queue.dma_start(target, result[:, :width])
             else:
-                queue.dma_start(target.rearrange("(i p) c -> p i c", p=P), result[:, :count, :])
+                queue.dma_start(target.rearrange("(i p) c -> p i c", p=P), result[:, :width].rearrange("p (i c) -> p i c", c=P))
 
-        def products(b):
+        def partners(b):
             name, index = blocks[b]
             others = [other for kind, other in blocks[:b] if kind != name]
-            pairs = [(index, other) if name == "x" else (other, index) for other in others]
-            if pairs:
-                bank = sum_bank()
-                product(bank, pairs, every, True, True)
-                store(bank, pairs, nc.scalar.copy, nc.sync)
-
-        def quantise_and_release(b):
-            quantise(b, every)
-            rooms.append(laid[b][:, : 2 * PASS])
-            scalar_lane()
+            return [(index, other) if name == "x" else (other, index) for other in others]
 
         every = range(PASSES)
+
+        def products(b):
+            if partners(b):
+                bank = take(free)
+                for i, (j, m) in enumerate(partners(b)):
+                    product(bank[:, i * P : (i + 1) * P], j, m, every, True, True)
+                store(bank, partners(b), nc.scalar.copy, nc.sync)
+
         scalar_lane()
         waiting = None
         for b in range(len(blocks)):
-            road = ROADS[b]
-            vector_gather_and_turn(b, 2 if road[2] == "C" else 3)
+            if b in THREE:
+                gather_rest(b)
+                turn_picked(b, 2)
+            else:
+                vector_gather_and_turn(b, 2)
             if waiting:
                 multiply_out(*waiting)
-                quantise_and_release(b - 1)
-            if road[2] == "B":
-                turn_picked(b, 2)
+                emptied.append(home[waiting])
+                quantise(b - 1, every)
+                release(laid[b - 1])
+            if b >= LATE:
                 turn_and_weave(b, 0, 2)
-                multiply_out(b, 3)
-                waiting = (b, 2)
-            else:
-                if b >= LATE:
-                    turn_and_weave(b, 0, 2)
-                vector_gather_and_turn(b, 3)
-                if b < LATE:
-                    turn_and_weave(b, 0, 2)
-                multiply_out(b, 2)
-                waiting = (b, 3)
-            if AHEAD <= b < last:
-                turn_and_weave(b + 1, 0, 2)
-            if b < last and ROADS[b + 1][2] == "B":
+            vector_gather_and_turn(b, 3)
+            if b < LATE:
+                turn_and_weave(b, 0, 2)
+            multiply_out(b, 2)
+            waiting = (b, 3)
+            if b + 1 in THREE:
                 gather_third(b + 1)
             if b >= 1:
                 products(b - 1)
-        m = DY_BLOCKS - 1
-        halves = [(sum_bank(), [(2 * h, m), (2 * h + 1, m)]) for h in range(2)]
-        quantise(last, range(2))
-        quantise(last, range(2, 3))
-        for bank, pairs in halves:
-            product(bank, pairs, range(3), True, False)
-        multiply_out(last, 3)
-        quantise(last, range(3, PASSES))
-        for bank, pairs in halves:
-            product(bank, pairs, range(3, PASSES), False, True)
+        halves = [(take(free), partners(last)[2 * h : 2 * h + 2]) for h in range(2)]
+        for passes in (range(2), [2], [3]):
+            if passes == [3]:
+                multiply_out(last, 3)
+            quantise(last, passes)
+            for bank, pairs in halves:
+                for i, (j, m) in enumerate(pairs):
+                    product(bank[:, i * P : (i + 1) * P], j, m, passes, i == 0 and passes[0] == 0, i == 1 and passes == [3])
         store(*halves[0], nc.vector.tensor_copy, nc.sync)
         store(*halves[1], nc.scalar.copy, nc.scalar)

@@ -29,8 +29,8 @@ DEALT = 3
 LATE = 3
 FIRST_BATCH = 2
 SPLIT = 1
-THREE = (3, 4, 6, 7, 9, 10)
-SHARE = 256
+THREE = (3, 4, 5, 6, 7, 8, 9, 10, 11)
+SHARE = 224
 ORDER = ["x", "dy"] * 4 + ["dy"] * 4
 
 
@@ -99,11 +99,14 @@ def tile_attend_gmw_kernel(tc, xT, dyT, sw, tw, offs, offs2, out):
         def scalar_gather(b, g, target):
             nc.scalar.activation(target, windows[b][:].indirect(offsets(b, g)), COPY)
 
+        def share(b):
+            return PASS if b == last else SHARE
+
         def gather_third(b):
             picked[b, 2] = take(v_slots)
             first = 2 * PASS // 16
             nc.scalar.activation(
-                picked[b, 2][:, :SHARE], windows[b][:].indirect(lists[blocks[b][0]][:, first : first + SHARE // 16]), COPY
+                picked[b, 2][:, : share(b)], windows[b][:].indirect(lists[blocks[b][0]][:, first : first + share(b) // 16]), COPY
             )
 
         def gather_rest(b):
@@ -119,9 +122,9 @@ def tile_attend_gmw_kernel(tc, xT, dyT, sw, tw, offs, offs2, out):
                     cols = slice(g * PASS, (g + 1) * PASS)
                     scalar_gather(b, g, pair[:, cols])
                     rounded[b, g] = room[:, cols]
-                    if b < SPLIT:
+                    if b < SPLIT or b == last:
                         nc.gpsimd.tensor_tensor(room[:, cols], pair[:, cols], rows[blocks[b][0]][:, cols], MULT)
-                if b >= SPLIT:
+                if SPLIT <= b < last:
                     nc.gpsimd.tensor_tensor(room, pair[:], rows[blocks[b][0]][:], MULT)
 
         def turn_and_weave(b, g, count):
@@ -221,7 +224,8 @@ def tile_attend_gmw_kernel(tc, xT, dyT, sw, tw, offs, offs2, out):
         waiting = None
         for b in range(len(blocks)):
             if b in THREE:
-                gather_rest(b)
+                if b < last:
+                    gather_rest(b)
                 turn_picked(b, 2)
             else:
                 vector_gather_and_turn(b, 2)
@@ -230,7 +234,10 @@ def tile_attend_gmw_kernel(tc, xT, dyT, sw, tw, offs, offs2, out):
                 emptied.append(home[waiting])
                 quantise(b - 1, every)
                 release(laid[b - 1])
-            if b >= LATE:
+            if b == last:
+                turn_and_weave(b, 0, 1)
+                turn_and_weave(b, 1, 1)
+            elif b >= LATE:
                 turn_and_weave(b, 0, 2)
             vector_gather_and_turn(b, 3)
             if b < LATE:
@@ -242,7 +249,7 @@ def tile_attend_gmw_kernel(tc, xT, dyT, sw, tw, offs, offs2, out):
             if b >= 1:
                 products(b - 1)
         halves = [(take(free), partners(last)[2 * h : 2 * h + 2]) for h in range(2)]
-        for passes in (range(2), [2], [3]):
+        for passes in ([0], [2], [1], [3]):
             if passes == [3]:
                 multiply_out(last, 3)
             quantise(last, passes)

@@ -18,47 +18,50 @@ MULT = mybir.AluOpType.mult
 COPY = mybir.ActivationFunctionType.Copy
 
 P = 128
-PASS = 512
+PASS = 4 * P
 PASSES = E // PASS
-WINDOW = 704
 X_BLOCKS = D // P
 DY_BLOCKS = DV // P
 BANKS = 8
-PICKED = 2
-DEALT = 3
-LATE = 3
-FIRST_BATCH = 2
-SPLIT = 1
-THREE = (3, 4, 5, 6, 7, 8, 9, 10, 11)
+OFFSETS_A_COLUMN = 16
+WINDOW = 2 * PASS + 16
+
+PAIR_TILES = 2
+DEALT_TILES = 3
+LEAD_IN = 3
 SHARE = 224
-ORDER = ["x", "dy"] * 4 + ["dy"] * 4
+RESULT_TILES = 4
+ROW_RESULT_TILES = 2
 
 
 def tile_attend_gmw_kernel(tc, xT, dyT, sw, tw, offs, offs2, out):
     nc = tc.nc
-    blocks = [(name, ORDER[:b].count(name)) for b, name in enumerate(ORDER)]
+    blocks = [(name, i) for i in range(X_BLOCKS) for name in ("x", "dy")] + [("dy", i) for i in range(X_BLOCKS, DY_BLOCKS)]
     table = {"x": xT, "dy": dyT}
     weights = {"x": sw, "dy": tw}
     last = len(blocks) - 1
 
     with ExitStack() as ctx:
         keep = ctx.enter_context(tc.tile_pool(name="keep", bufs=1))
-        ring = ctx.enter_context(tc.tile_pool(name="ring", bufs=3))
+        ring = ctx.enter_context(tc.tile_pool(name="ring", bufs=RESULT_TILES))
         psum = ctx.enter_context(tc.psum_pool(name="psum", bufs=1))
 
-        lists = {name: keep.tile([P, E // 16], U16, name="list_" + name) for name in ("x", "dy")}
+        lists = {name: keep.tile([P, E // OFFSETS_A_COLUMN], U16, name="list_" + name) for name in ("x", "dy")}
         rows = {name: keep.tile([P, 2 * PASS], F32, name="rows_" + name) for name in ("x", "dy")}
         columns = {name: keep.tile([P, 2, 4], F32, name="columns_" + name) for name in ("x", "dy")}
-        windows = [keep.tile([P, WINDOW], F32, name="window%d" % b) for b in range(len(blocks))]
+        window_tiles = {
+            name: [keep.tile([P, WINDOW], F32, name="window_%s%d" % (name, i)) for i in range(count // 2)]
+            for name, count in (("x", X_BLOCKS), ("dy", DY_BLOCKS))
+        }
+        windows = [window_tiles[name][i % len(window_tiles[name])] for name, i in blocks]
+        first_use = [b for b, (name, i) in enumerate(blocks) if i < len(window_tiles[name])]
         ident = keep.tile([P, P], F32, name="ident")
         free = [psum.tile([P, PASS], F32, name="bank%d" % i) for i in range(BANKS)]
 
         def load_block(b):
             name, block = blocks[b]
-            nc.sync.dma_start(windows[b][:, :V], table[name][block * P : (block + 1) * P, :])
-
-        def load_columns(name):
-            nc.sync.dma_start(columns[name][:], weights[name][0:1, 2 * PASS :].rearrange("o (g p t) -> p (o g) t", p=P, t=4))
+            queue = nc.scalar if b == 0 else nc.sync
+            queue.dma_start(windows[b][:, :V], table[name][block * P : (block + 1) * P, :])
 
         def load_rows(name, g):
             nc.sync.dma_start(rows[name][:, g * PASS : (g + 1) * PASS], weights[name][:, g * PASS : (g + 1) * PASS])
@@ -67,13 +70,13 @@ def tile_attend_gmw_kernel(tc, xT, dyT, sw, tw, offs, offs2, out):
             nc.sync.dma_start(lists[name][:], index_list)
             load_block(b)
             load_rows(name, 0)
-            load_columns(name)
+            nc.sync.dma_start(columns[name][:], weights[name][0:1, 2 * PASS :].rearrange("o (g p t) -> p (o g) t", p=P, t=4))
             load_rows(name, 1)
-        for b in range(2, len(blocks)):
+        for b in first_use[2:]:
             load_block(b)
 
-        for window in windows:
-            nc.vector.memset(window[:, V:].bitcast(I32), 0)
+        for b in first_use:
+            nc.vector.memset(windows[b][:, V:].bitcast(I32), 0)
         make_identity(nc, ident[:])
         warm = keep.tile([P, 1], F32, name="warm")
         nc.scalar.activation(warm[:], windows[0][:, V : V + 1], COPY)
@@ -81,91 +84,72 @@ def tile_attend_gmw_kernel(tc, xT, dyT, sw, tw, offs, offs2, out):
         laid = [keep.tile([P, E], BF16, name="laid%d" % b, align_bytes=64) for b in range(len(blocks))]
         codes = {key: keep.tile([P, PASSES * P], U32, name="codes_%s%d" % key, align_bytes=64) for key in blocks}
         scales = {key: keep.tile([P, PASSES * P], U8, name="scales_%s%d" % key, align_bytes=64) for key in blocks}
-        s_slots = [keep.tile([P, 2 * PASS], F32, name="s_slot%d" % i) for i in range(PICKED)]
-        v_slots = [keep.tile([P, PASS], F32, name="v_slot%d" % i) for i in range(DEALT)]
+        pair_tiles = [keep.tile([P, 2 * PASS], F32, name="pair%d" % i) for i in range(PAIR_TILES)]
+        dealt_tiles = [keep.tile([P, PASS], F32, name="dealt%d" % i) for i in range(DEALT_TILES)]
 
-        def offsets(b, g):
-            return lists[blocks[b][0]][:, g * PASS // 16 : (g + 1) * PASS // 16]
+        shared, rounded, turned = {}, {}, {}
 
-        picked, rounded, turned, home = {}, {}, {}, {}
-        emptied = []
-        rooms = [keep.tile([P, 2 * PASS], BF16, name="room%d" % i)[:] for i in range(FIRST_BATCH)]
-        units = list(range(len(blocks)))
+        def take(tiles):
+            tiles.append(tiles.pop(0))
+            return tiles[-1]
 
-        def take(slots):
-            slots.append(slots.pop(0))
-            return slots[-1]
+        def gathered(b, first, count, dtype=F32):
+            offsets = lists[blocks[b][0]][:, first // OFFSETS_A_COLUMN : (first + count) // OFFSETS_A_COLUMN]
+            return (windows[b][:] if dtype is F32 else windows[b][:].bitcast(dtype)).indirect(offsets)
 
-        def scalar_gather(b, g, target):
-            nc.scalar.activation(target, windows[b][:].indirect(offsets(b, g)), COPY)
+        def gather_and_multiply_pair(b, room):
+            pair = take(pair_tiles)
+            in_halves = b in (0, last)
+            for g in range(2):
+                cols = slice(g * PASS, (g + 1) * PASS)
+                rounded[b, g] = room[:, cols]
+                if in_halves:
+                    nc.scalar.activation(pair[:, cols], gathered(b, g * PASS, PASS), COPY)
+                    nc.gpsimd.tensor_tensor(room[:, cols], pair[:, cols], rows[blocks[b][0]][:, cols], MULT)
+            if not in_halves:
+                nc.scalar.activation(pair[:], gathered(b, 0, 2 * PASS), COPY)
+                nc.gpsimd.tensor_tensor(room, pair[:], rows[blocks[b][0]][:], MULT)
 
-        def share(b):
-            return PASS if b == last else SHARE
-
-        def gather_third(b):
-            picked[b, 2] = take(v_slots)
-            first = 2 * PASS // 16
-            nc.scalar.activation(
-                picked[b, 2][:, : share(b)], windows[b][:].indirect(lists[blocks[b][0]][:, first : first + share(b) // 16]), COPY
-            )
-
-        def gather_rest(b):
-            first = (2 * PASS + SHARE) // 16
-            nc.vector.tensor_copy(picked[b, 2][:, SHARE:], windows[b][:].indirect(lists[blocks[b][0]][:, first : 3 * PASS // 16]))
-
-        def scalar_lane():
-            while rooms and units:
-                b = units.pop(0)
-                pair = take(s_slots)
-                room = rooms.pop(0)
-                for g in range(2):
-                    cols = slice(g * PASS, (g + 1) * PASS)
-                    scalar_gather(b, g, pair[:, cols])
-                    rounded[b, g] = room[:, cols]
-                    if b < SPLIT or b == last:
-                        nc.gpsimd.tensor_tensor(room[:, cols], pair[:, cols], rows[blocks[b][0]][:, cols], MULT)
-                if SPLIT <= b < last:
-                    nc.gpsimd.tensor_tensor(room, pair[:], rows[blocks[b][0]][:], MULT)
-
-        def turn_and_weave(b, g, count):
-            whole = emptied.pop() if emptied else free[0]
-            free.remove(whole)
-            free.append(whole)
-            bank = whole[:].rearrange("p (c u i) -> p c u i", u=2, i=2)
+        def turn_words(b, g, count, bank):
+            free.remove(bank)
+            free.append(bank)
+            view = bank[:].rearrange("p (c u i) -> p c u i", u=2, i=2)
             for k in range(count):
                 words = rounded[b, g + k].bitcast(F32)
                 for u in range(2):
-                    nc.tensor.transpose(bank[:, k * P // 2 : (k + 1) * P // 2, u, :], words[:, u : 2 * P : 2], ident[:])
+                    nc.tensor.transpose(view[:, k * P // 2 : (k + 1) * P // 2, u, :], words[:, u : 2 * P : 2], ident[:])
             nc.scalar.copy(
                 laid[b][:, g * PASS : (g + count) * PASS].bitcast(F32).rearrange("p (c i u) -> p c u i", i=2, u=2),
-                bank[:, : count * P // 2],
+                view[:, : count * P // 2],
             )
 
-        def turn_bank(b, g):
-            home[b, g] = take(free)
-            turned[b, g] = home[b, g][:].rearrange("p (c t i) -> p c t i", t=4, i=2)
-            return turned[b, g]
+        def places(bank):
+            return bank[:].rearrange("p (c t i) -> p c t i", t=4, i=2)
 
-        def vector_gather_and_turn(b, g):
-            dealt = take(v_slots)
-            nc.vector.tensor_copy(
-                dealt[:].bitcast(U32).rearrange("f (u s w) -> f s u w", u=2, w=2),
-                windows[b][:].bitcast(U32).indirect(offsets(b, g)),
-            )
-            bank = turn_bank(b, g)
+        def deal_and_turn(b, g):
+            dealt = take(dealt_tiles)
+            nc.vector.tensor_copy(dealt[:].bitcast(U32).rearrange("f (u s w) -> f s u w", u=2, w=2), gathered(b, g * PASS, PASS, U32))
+            turned[b, g] = take(free)
             for u in range(2):
                 for w in range(2):
-                    nc.tensor.transpose(bank[:, :, 2 * u + w, :], dealt[:, 2 * P * u + w : 2 * P * (u + 1) : 2], ident[:])
+                    nc.tensor.transpose(places(turned[b, g])[:, :, 2 * u + w, :], dealt[:, 2 * P * u + w : 2 * P * (u + 1) : 2], ident[:])
 
-        def turn_picked(b, g):
-            bank = turn_bank(b, g)
+        def gather_scalars_share(b):
+            count = PASS if b == last else SHARE
+            shared[b] = take(dealt_tiles)
+            nc.scalar.activation(shared[b][:, :count], gathered(b, 2 * PASS, count), COPY)
+
+        def finish_shared_and_turn(b):
+            if b < last:
+                nc.vector.tensor_copy(shared[b][:, SHARE:], gathered(b, 2 * PASS + SHARE, PASS - SHARE))
+            turned[b, 2] = take(free)
             for t in range(4):
-                nc.tensor.transpose(bank[:, :, t, :], picked[b, g][:, t:PASS:4], ident[:])
+                nc.tensor.transpose(places(turned[b, 2])[:, :, t, :], shared[b][:, t:PASS:4], ident[:])
 
         def multiply_out(b, g):
             nc.vector.tensor_tensor(
                 laid[b][:, g * PASS : (g + 1) * PASS].rearrange("p (c i t) -> p c t i", i=2, t=4),
-                turned[b, g],
+                places(turned[b, g]),
                 columns[blocks[b][0]][:, g - 2 : g - 1, :].unsqueeze(3).to_broadcast([P, P // 2, 4, 2]),
                 MULT,
             )
@@ -177,10 +161,6 @@ def tile_attend_gmw_kernel(tc, xT, dyT, sw, tw, offs, offs2, out):
                 scales=scales[blocks[b]][:, cols],
                 in_=laid[b][:, 4 * cols.start : 4 * cols.stop],
             )
-
-        def release(spent):
-            rooms.append(spent[:, : 2 * PASS])
-            scalar_lane()
 
         def product(target, j, m, passes, opens, closes):
             for g in passes:
@@ -195,66 +175,69 @@ def tile_attend_gmw_kernel(tc, xT, dyT, sw, tw, offs, offs2, out):
                     stop=(closes and g == passes[-1]),
                 )
 
-        def store(bank, pairs, copy, queue):
-            width = len(pairs) * P
-            result = ring.tile([P, PASS], F32, name="result", bufs=4)
-            copy(result[:, :width], bank[:, :width])
-            (j, m), (j_end, m_end) = pairs[0], pairs[-1]
-            target = out[j * P : (j_end + 1) * P, m * P : (m_end + 1) * P]
-            if j_end == j:
-                queue.dma_start(target, result[:, :width])
-            else:
-                queue.dma_start(target.rearrange("(i p) c -> p i c", p=P), result[:, :width].rearrange("p (i c) -> p i c", c=P))
-
-        def partners(b):
-            name, index = blocks[b]
-            others = [other for kind, other in blocks[:b] if kind != name]
-            return [(index, other) if name == "x" else (other, index) for other in others]
+        def store_column(bank, first, count, m, copy, queue):
+            result = ring.tile([P, X_BLOCKS, P], F32, name="result")
+            target = out[first * P : (first + count) * P, m * P : (m + 1) * P].rearrange("(i p) c -> p i c", p=P)
+            copy(result[:, :count].rearrange("p i c -> p (i c)"), bank[:, : count * P])
+            queue.dma_start(target, result[:, :count])
 
         every = range(PASSES)
+        row_banks = [free.pop() for j in range(X_BLOCKS)]
+        row_results = [keep.tile([P, PASS], F32, name="row_result%d" % i) for i in range(ROW_RESULT_TILES)]
 
         def products(b):
-            if partners(b):
-                bank = take(free)
-                for i, (j, m) in enumerate(partners(b)):
-                    product(bank[:, i * P : (i + 1) * P], j, m, every, True, True)
-                store(bank, partners(b), nc.scalar.copy, nc.sync)
+            name, index = blocks[b]
+            if index >= X_BLOCKS:
+                bank = take(row_banks)
+                for j in range(X_BLOCKS):
+                    product(bank[:, j * P : (j + 1) * P], j, index, every, True, True)
+                store_column(bank, 0, X_BLOCKS, index, nc.scalar.copy, nc.sync)
+                return
+            for kind, other in blocks[:b]:
+                if kind != name:
+                    j, m = (index, other) if name == "x" else (other, index)
+                    product(row_banks[j][:, m * P : (m + 1) * P], j, m, every, True, True)
+            if blocks[b] == ("dy", X_BLOCKS - 1):
+                for j in range(X_BLOCKS):
+                    result = row_results[j % ROW_RESULT_TILES]
+                    nc.scalar.copy(result[:], row_banks[j][:])
+                    nc.sync.dma_start(out[j * P : (j + 1) * P, : X_BLOCKS * P], result[:])
 
-        scalar_lane()
-        waiting = None
+        for b in range(PAIR_TILES):
+            gather_and_multiply_pair(b, keep.tile([P, 2 * PASS], BF16, name="first_rounded%d" % b)[:])
         for b in range(len(blocks)):
-            if b in THREE:
-                if b < last:
-                    gather_rest(b)
-                turn_picked(b, 2)
+            if b >= LEAD_IN:
+                finish_shared_and_turn(b)
             else:
-                vector_gather_and_turn(b, 2)
-            if waiting:
-                multiply_out(*waiting)
-                emptied.append(home[waiting])
+                deal_and_turn(b, 2)
+            if b >= 1:
+                multiply_out(b - 1, 3)
                 quantise(b - 1, every)
-                release(laid[b - 1])
+                if b < last:
+                    gather_and_multiply_pair(b + 1, laid[b - 1][:, : 2 * PASS])
             if b == last:
-                turn_and_weave(b, 0, 1)
-                turn_and_weave(b, 1, 1)
-            elif b >= LATE:
-                turn_and_weave(b, 0, 2)
-            vector_gather_and_turn(b, 3)
-            if b < LATE:
-                turn_and_weave(b, 0, 2)
+                turn_words(b, 0, 1, turned[b - 1, 3])
+                turn_words(b, 1, 1, free[0])
+            elif b >= LEAD_IN:
+                turn_words(b, 0, 2, turned[b - 1, 3])
+            deal_and_turn(b, 3)
+            for later in range(b + 1, len(blocks)):
+                if windows[later] is windows[b]:
+                    load_block(later)
+            if b < LEAD_IN:
+                turn_words(b, 0, 2, turned[b - 1, 3] if b else free[0])
             multiply_out(b, 2)
-            waiting = (b, 3)
-            if b + 1 in THREE:
-                gather_third(b + 1)
+            if LEAD_IN <= b + 1 <= last:
+                gather_scalars_share(b + 1)
             if b >= 1:
                 products(b - 1)
-        halves = [(take(free), partners(last)[2 * h : 2 * h + 2]) for h in range(2)]
-        for passes in ([0], [2], [1], [3]):
-            if passes == [3]:
+
+        halves = [take(row_banks) for h in range(2)]
+        for g in (0, 2, 1, 3):
+            if g == 3:
                 multiply_out(last, 3)
-            quantise(last, passes)
-            for bank, pairs in halves:
-                for i, (j, m) in enumerate(pairs):
-                    product(bank[:, i * P : (i + 1) * P], j, m, passes, i == 0 and passes[0] == 0, i == 1 and passes == [3])
-        store(*halves[0], nc.vector.tensor_copy, nc.sync)
-        store(*halves[1], nc.scalar.copy, nc.scalar)
+            quantise(last, [g])
+            for j in range(X_BLOCKS):
+                product(halves[j // 2][:, (j % 2) * P : (j % 2 + 1) * P], j, DY_BLOCKS - 1, [g], j % 2 == 0 and g == 0, j % 2 == 1 and g == 3)
+        store_column(halves[0], 0, 2, DY_BLOCKS - 1, nc.vector.tensor_copy, nc.sync)
+        store_column(halves[1], 2, 2, DY_BLOCKS - 1, nc.scalar.copy, nc.scalar)

@@ -100,24 +100,36 @@ def tile_attend_gmw_kernel(tc, xT, dyT, sw, tw, offs, offs2, out):
         def gather_and_multiply_pair(b, room):
             pair = take(pair_tiles)
             in_halves = b in (0, last)
-            for g in range(2):
-                cols = slice(g * PASS, (g + 1) * PASS)
-                rounded[b, g] = room[:, cols]
-                if in_halves:
+            row = rows[blocks[b][0]]
+            if in_halves:
+                for g in range(2):
+                    cols = slice(g * PASS, (g + 1) * PASS)
+                    rounded[b, g] = [room[:, g * PASS + u * 2 * P : g * PASS + (u + 1) * 2 * P] for u in range(2)]
                     nc.scalar.activation(pair[:, cols], gathered(b, g * PASS, PASS), COPY)
-                    nc.gpsimd.tensor_tensor(room[:, cols], pair[:, cols], rows[blocks[b][0]][:, cols], MULT)
-            if not in_halves:
+                    nc.gpsimd.tensor_tensor(
+                        room[:, cols].rearrange("p (u q j) -> p q u j", u=2, j=16),
+                        pair[:, cols].rearrange("p (q u j) -> p q u j", u=2, j=16),
+                        row[:, cols].rearrange("p (q u j) -> p q u j", u=2, j=16),
+                        MULT,
+                    )
+            else:
+                for g in range(2):
+                    rounded[b, g] = [room[:, u * PASS + g * 2 * P : u * PASS + (g + 1) * 2 * P] for u in range(2)]
                 nc.scalar.activation(pair[:], gathered(b, 0, 2 * PASS), COPY)
-                nc.gpsimd.tensor_tensor(room, pair[:], rows[blocks[b][0]][:], MULT)
+                nc.gpsimd.tensor_tensor(
+                    room.rearrange("p (u q j) -> p q u j", u=2, j=16),
+                    pair[:].rearrange("p (q u j) -> p q u j", u=2, j=16),
+                    row[:].rearrange("p (q u j) -> p q u j", u=2, j=16),
+                    MULT,
+                )
 
         def turn_words(b, g, count, bank):
             free.remove(bank)
             free.append(bank)
             view = bank[:].rearrange("p (c u i) -> p c u i", u=2, i=2)
             for k in range(count):
-                words = rounded[b, g + k].bitcast(F32)
                 for u in range(2):
-                    nc.tensor.transpose(view[:, k * P // 2 : (k + 1) * P // 2, u, :], words[:, u : 2 * P : 2], ident[:])
+                    nc.tensor.transpose(view[:, k * P // 2 : (k + 1) * P // 2, u, :], rounded[b, g + k][u].bitcast(F32), ident[:])
             nc.scalar.copy(
                 laid[b][:, g * PASS : (g + count) * PASS].bitcast(F32).rearrange("p (c i u) -> p c u i", i=2, u=2),
                 view[:, : count * P // 2],
@@ -128,11 +140,10 @@ def tile_attend_gmw_kernel(tc, xT, dyT, sw, tw, offs, offs2, out):
 
         def deal_and_turn(b, g):
             dealt = take(dealt_tiles)
-            nc.vector.tensor_copy(dealt[:].bitcast(U32).rearrange("f (u s w) -> f s u w", u=2, w=2), gathered(b, g * PASS, PASS, U32))
+            nc.vector.tensor_copy(dealt[:].bitcast(U32).rearrange("f (t s) -> f s t", t=4), gathered(b, g * PASS, PASS, U32))
             turned[b, g] = take(free)
-            for u in range(2):
-                for w in range(2):
-                    nc.tensor.transpose(places(turned[b, g])[:, :, 2 * u + w, :], dealt[:, 2 * P * u + w : 2 * P * (u + 1) : 2], ident[:])
+            for t in range(4):
+                nc.tensor.transpose(places(turned[b, g])[:, :, t, :], dealt[:, t * P : (t + 1) * P], ident[:])
 
         def gather_scalars_share(b):
             count = PASS if b == last else SHARE

@@ -29,7 +29,7 @@ WINDOW = 2 * PASS + 16
 PAIR_TILES = 2
 DEALT_TILES = 3
 LEAD_IN = 3
-SHARE = 224
+SHARE = 256
 RESULT_TILES = 4
 ROW_RESULT_TILES = 2
 
@@ -60,8 +60,7 @@ def tile_attend_gmw_kernel(tc, xT, dyT, sw, tw, offs, offs2, out):
 
         def load_block(b):
             name, block = blocks[b]
-            queue = nc.scalar if b == 0 else nc.sync
-            queue.dma_start(windows[b][:, :V], table[name][block * P : (block + 1) * P, :])
+            nc.sync.dma_start(windows[b][:, :V], table[name][block * P : (block + 1) * P, :])
 
         def load_rows(name, g):
             nc.sync.dma_start(rows[name][:, g * PASS : (g + 1) * PASS], weights[name][:, g * PASS : (g + 1) * PASS])

@@ -74,11 +74,12 @@ def tile_attend_gmw_kernel(tc, xT, dyT, sw, tw, offs, offs2, out):
         for b in first_use[2:]:
             load_block(b)
 
+        cold, warm = keep.tile([P, 1], F32, name="cold"), keep.tile([P, 1], F32, name="warm")
+        nc.gpsimd.memset(cold[:], 0.0)
+        nc.scalar.activation(warm[:], cold[:], COPY)
         for b in first_use:
             nc.vector.memset(windows[b][:, V:].bitcast(I32), 0)
         make_identity(nc, ident[:])
-        warm = keep.tile([P, 1], F32, name="warm")
-        nc.scalar.activation(warm[:], windows[0][:, V : V + 1], COPY)
 
         laid = [keep.tile([P, E], BF16, name="laid%d" % b, align_bytes=64) for b in range(len(blocks))]
         codes = {key: keep.tile([P, PASSES * P], U32, name="codes_%s%d" % key, align_bytes=64) for key in blocks}

@@ -29,7 +29,7 @@ WINDOW = 2 * PASS + 16
 PAIR_TILES = 2
 DEALT_TILES = 3
 LEAD_IN = 3
-SHARE = 256
+SHARE = 288
 RESULT_TILES = 4
 ROW_RESULT_TILES = 2
 

@@ -29,7 +29,7 @@ WINDOW = 2 * PASS + 16
 PAIR_TILES = 2
 DEALT_TILES = 3
 LEAD_IN = 3
-SHARE = 288
+SHARES = (256, 288)
 RESULT_TILES = 4
 ROW_RESULT_TILES = 2
 
@@ -146,13 +146,14 @@ def tile_attend_gmw_kernel(tc, xT, dyT, sw, tw, offs, offs2, out):
                 nc.tensor.transpose(places(turned[b, g])[:, :, t, :], dealt[:, t * P : (t + 1) * P], ident[:])
 
         def gather_scalars_share(b):
-            count = PASS if b == last else SHARE
+            count = PASS if b == last else SHARES[b % 2]
             shared[b] = take(dealt_tiles)
             nc.scalar.activation(shared[b][:, :count], gathered(b, 2 * PASS, count), COPY)
 
         def finish_shared_and_turn(b):
             if b < last:
-                nc.vector.tensor_copy(shared[b][:, SHARE:], gathered(b, 2 * PASS + SHARE, PASS - SHARE))
+                share = SHARES[b % 2]
+                nc.vector.tensor_copy(shared[b][:, share:], gathered(b, 2 * PASS + share, PASS - share))
             turned[b, 2] = take(free)
             for t in range(4):
                 nc.tensor.transpose(places(turned[b, 2])[:, :, t, :], shared[b][:, t:PASS:4], ident[:])

from contextlib import ExitStack

import concourse.mybir as mybir
from concourse.masks import make_identity

V, E, D, DV = 512, 2048, 512, 1024
FLOPS = 2 * E * D * DV

F32 = mybir.dt.float32
BF16 = mybir.dt.bfloat16
I32 = mybir.dt.int32
U32 = mybir.dt.uint32
U16 = mybir.dt.uint16
U8 = mybir.dt.uint8
E4M3 = mybir.dt.float8_e4m3fn_x4
E5M2 = mybir.dt.float8_e5m2_x4
MULT = mybir.AluOpType.mult
COPY = mybir.ActivationFunctionType.Copy

P = 128
PASS = 4 * P
PASSES = E // PASS
X_BLOCKS = D // P
DY_BLOCKS = DV // P
BANKS = 8
OFFSETS_A_COLUMN = 16
WINDOW = 2 * PASS + 16

PAIR_TILES = 2
DEALT_TILES = 3
LEAD_IN = 3
SHARES = (256, 288)
RESULT_TILES = 4
ROW_RESULT_TILES = 2


def tile_attend_gmw_kernel(tc, xT, dyT, sw, tw, offs, offs2, out):
    nc = tc.nc
    blocks = [(name, i) for i in range(X_BLOCKS) for name in ("x", "dy")] + [("dy", i) for i in range(X_BLOCKS, DY_BLOCKS)]
    table = {"x": xT, "dy": dyT}
    weights = {"x": sw, "dy": tw}
    last = len(blocks) - 1

    with ExitStack() as ctx:
        keep = ctx.enter_context(tc.tile_pool(name="keep", bufs=1))
        ring = ctx.enter_context(tc.tile_pool(name="ring", bufs=RESULT_TILES))
        psum = ctx.enter_context(tc.psum_pool(name="psum", bufs=1))

        lists = {name: keep.tile([P, E // OFFSETS_A_COLUMN], U16, name="list_" + name) for name in ("x", "dy")}
        rows = {name: keep.tile([P, 2 * PASS], F32, name="rows_" + name) for name in ("x", "dy")}
        columns = {name: keep.tile([P, 2, 4], F32, name="columns_" + name) for name in ("x", "dy")}
        window_tiles = {
            name: [keep.tile([P, WINDOW], F32, name="window_%s%d" % (name, i)) for i in range(count // 2)]
            for name, count in (("x", X_BLOCKS), ("dy", DY_BLOCKS))
        }
        windows = [window_tiles[name][i % len(window_tiles[name])] for name, i in blocks]
        first_use = [b for b, (name, i) in enumerate(blocks) if i < len(window_tiles[name])]
        ident = keep.tile([P, P], F32, name="ident")
        free = [psum.tile([P, PASS], F32, name="bank%d" % i) for i in range(BANKS)]

        def load_block(b):
            name, block = blocks[b]
            nc.sync.dma_start(windows[b][:, :V], table[name][block * P : (block + 1) * P, :])

        def load_rows(name, g):
            nc.sync.dma_start(rows[name][:, g * PASS : (g + 1) * PASS], weights[name][:, g * PASS : (g + 1) * PASS])

        for b, (name, index_list) in enumerate((("x", offs), ("dy", offs2))):
            nc.sync.dma_start(lists[name][:], index_list)
            load_block(b)
            load_rows(name, 0)
            nc.sync.dma_start(columns[name][:], weights[name][0:1, 2 * PASS :].rearrange("o (g p t) -> p (o g) t", p=P, t=4))
            load_rows(name, 1)
        for b in first_use[2:]:
            load_block(b)

        cold, warm = keep.tile([P, 1], F32, name="cold"), keep.tile([P, 1], F32, name="warm")
        nc.gpsimd.memset(cold[:], 0.0)
        nc.scalar.activation(warm[:], cold[:], COPY)
        for b in first_use:
            nc.vector.memset(windows[b][:, V:].bitcast(I32), 0)
        make_identity(nc, ident[:])

        laid = [keep.tile([P, E], BF16, name="laid%d" % b, align_bytes=64) for b in range(len(blocks))]
        codes = {key: keep.tile([P, PASSES * P], U32, name="codes_%s%d" % key, align_bytes=64) for key in blocks}
        scales = {key: keep.tile([P, PASSES * P], U8, name="scales_%s%d" % key, align_bytes=64) for key in blocks}
        pair_tiles = [keep.tile([P, 2 * PASS], F32, name="pair%d" % i) for i in range(PAIR_TILES)]
        dealt_tiles = [keep.tile([P, PASS], F32, name="dealt%d" % i) for i in range(DEALT_TILES)]

        shared, rounded, turned = {}, {}, {}

        def take(tiles):
            tiles.append(tiles.pop(0))
            return tiles[-1]

        def gathered(b, first, count, dtype=F32):
            offsets = lists[blocks[b][0]][:, first // OFFSETS_A_COLUMN : (first + count) // OFFSETS_A_COLUMN]
            return (windows[b][:] if dtype is F32 else windows[b][:].bitcast(dtype)).indirect(offsets)

        def gather_and_multiply_pair(b, room):
            pair = take(pair_tiles)
            in_halves = b in (0, last)
            row = rows[blocks[b][0]]
            if in_halves:
                for g in range(2):
                    cols = slice(g * PASS, (g + 1) * PASS)
                    rounded[b, g] = [room[:, g * PASS + u * 2 * P : g * PASS + (u + 1) * 2 * P] for u in range(2)]
                    nc.scalar.activation(pair[:, cols], gathered(b, g * PASS, PASS), COPY)
                    nc.gpsimd.tensor_tensor(
                        room[:, cols].rearrange("p (u q j) -> p q u j", u=2, j=16),
                        pair[:, cols].rearrange("p (q u j) -> p q u j", u=2, j=16),
                        row[:, cols].rearrange("p (q u j) -> p q u j", u=2, j=16),
                        MULT,
                    )
            else:
                for g in range(2):
                    rounded[b, g] = [room[:, u * PASS + g * 2 * P : u * PASS + (g + 1) * 2 * P] for u in range(2)]
                nc.scalar.activation(pair[:], gathered(b, 0, 2 * PASS), COPY)
                nc.gpsimd.tensor_tensor(
                    room.rearrange("p (u q j) -> p q u j", u=2, j=16),
                    pair[:].rearrange("p (q u j) -> p q u j", u=2, j=16),
                    row[:].rearrange("p (q u j) -> p q u j", u=2, j=16),
                    MULT,
                )

        def turn_words(b, g, count, bank):
            free.remove(bank)
            free.append(bank)
            view = bank[:].rearrange("p (c u i) -> p c u i", u=2, i=2)
            for k in range(count):
                for u in range(2):
                    nc.tensor.transpose(view[:, k * P // 2 : (k + 1) * P // 2, u, :], rounded[b, g + k][u].bitcast(F32), ident[:])
            nc.scalar.copy(
                laid[b][:, g * PASS : (g + count) * PASS].bitcast(F32).rearrange("p (c i u) -> p c u i", i=2, u=2),
                view[:, : count * P // 2],
            )

        def places(bank):
            return bank[:].rearrange("p (c t i) -> p c t i", t=4, i=2)

        def deal_and_turn(b, g):
            dealt = take(dealt_tiles)
            nc.vector.tensor_copy(dealt[:].bitcast(U32).rearrange("f (t s) -> f s t", t=4), gathered(b, g * PASS, PASS, U32))
            turned[b, g] = take(free)
            for t in range(4):
                nc.tensor.transpose(places(turned[b, g])[:, :, t, :], dealt[:, t * P : (t + 1) * P], ident[:])

        def gather_scalars_share(b):
            count = PASS if b == last else SHARES[b % 2]
            shared[b] = take(dealt_tiles)
            nc.scalar.activation(shared[b][:, :count], gathered(b, 2 * PASS, count), COPY)

        def finish_shared_and_turn(b):
            if b < last:
                share = SHARES[b % 2]
                nc.vector.tensor_copy(shared[b][:, share:], gathered(b, 2 * PASS + share, PASS - share))
            turned[b, 2] = take(free)
            for t in range(4):
                nc.tensor.transpose(places(turned[b, 2])[:, :, t, :], shared[b][:, t:PASS:4], ident[:])

        def multiply_out(b, g):
            nc.vector.tensor_tensor(
                laid[b][:, g * PASS : (g + 1) * PASS].rearrange("p (c i t) -> p c t i", i=2, t=4),
                places(turned[b, g]),
                columns[blocks[b][0]][:, g - 2 : g - 1, :].unsqueeze(3).to_broadcast([P, P // 2, 4, 2]),
                MULT,
            )

        def quantise(b, passes):
            cols = slice(passes[0] * P, (passes[-1] + 1) * P)
            nc.vector.quantize_mx(
                out=codes[blocks[b]][:, cols].bitcast(E4M3 if blocks[b][0] == "x" else E5M2),
                scales=scales[blocks[b]][:, cols],
                in_=laid[b][:, 4 * cols.start : 4 * cols.stop],
            )

        def product(target, j, m, passes, opens, closes):
            for g in passes:
                cols = slice(g * P, (g + 1) * P)
                nc.tensor.matmul_mx(
                    out=target,
                    lhsT=codes["x", j][:, cols].bitcast(E4M3),
                    lhsT_scale=scales["x", j][:, cols],
                    rhs=codes["dy", m][:, cols].bitcast(E5M2),
                    rhs_scale=scales["dy", m][:, cols],
                    start=(opens and g == passes[0]),
                    stop=(closes and g == passes[-1]),
                )

        def store_column(bank, first, count, m, copy, queue):
            result = ring.tile([P, X_BLOCKS, P], F32, name="result")
            target = out[first * P : (first + count) * P, m * P : (m + 1) * P].rearrange("(i p) c -> p i c", p=P)
            copy(result[:, :count].rearrange("p i c -> p (i c)"), bank[:, : count * P])
            queue.dma_start(target, result[:, :count])

        every = range(PASSES)
        row_banks = [free.pop() for j in range(X_BLOCKS)]
        row_results = [keep.tile([P, PASS], F32, name="row_result%d" % i) for i in range(ROW_RESULT_TILES)]

        def products(b):
            name, index = blocks[b]
            if index >= X_BLOCKS:
                bank = take(row_banks)
                for j in range(X_BLOCKS):
                    product(bank[:, j * P : (j + 1) * P], j, index, every, True, True)
                store_column(bank, 0, X_BLOCKS, index, nc.scalar.copy, nc.sync)
                return
            for kind, other in blocks[:b]:
                if kind != name:
                    j, m = (index, other) if name == "x" else (other, index)
                    product(row_banks[j][:, m * P : (m + 1) * P], j, m, every, True, True)
            if blocks[b] == ("dy", X_BLOCKS - 1):
                for j in range(X_BLOCKS):
                    result = row_results[j % ROW_RESULT_TILES]
                    nc.scalar.copy(result[:], row_banks[j][:])
                    nc.sync.dma_start(out[j * P : (j + 1) * P, : X_BLOCKS * P], result[:])

        for b in range(PAIR_TILES):
            gather_and_multiply_pair(b, keep.tile([P, 2 * PASS], BF16, name="first_rounded%d" % b)[:])
        for b in range(len(blocks)):
            if b >= LEAD_IN:
                finish_shared_and_turn(b)
            else:
                deal_and_turn(b, 2)
            if b >= 1:
                multiply_out(b - 1, 3)
                quantise(b - 1, every)
                if b < last:
                    gather_and_multiply_pair(b + 1, laid[b - 1][:, : 2 * PASS])
            if b == last:
                turn_words(b, 0, 1, turned[b - 1, 3])
                turn_words(b, 1, 1, free[0])
            elif b >= LEAD_IN:
                turn_words(b, 0, 2, turned[b - 1, 3])
            deal_and_turn(b, 3)
            for later in range(b + 1, len(blocks)):
                if windows[later] is windows[b]:
                    load_block(later)
            if b < LEAD_IN:
                turn_words(b, 0, 2, turned[b - 1, 3] if b else free[0])
            multiply_out(b, 2)
            if LEAD_IN <= b + 1 <= last:
                gather_scalars_share(b + 1)
            if b >= 1:
                products(b - 1)

        halves = [take(row_banks) for h in range(2)]
        for g in (0, 2, 1, 3):
            if g == 3:
                multiply_out(last, 3)
            quantise(last, [g])
            for j in range(X_BLOCKS):
                product(halves[j // 2][:, (j % 2) * P : (j % 2 + 1) * P], j, DY_BLOCKS - 1, [g], j % 2 == 0 and g == 0, j % 2 == 1 and g == 3)
        store_column(halves[0], 0, 2, DY_BLOCKS - 1, nc.vector.tensor_copy, nc.sync)
        store_column(halves[1], 2, 2, DY_BLOCKS - 1, nc.scalar.copy, nc.scalar)
